import numpy as np
import ml_dtypes


def mxq(x, axis, fmt="e4m3"):
    dtype, down = {"e4m3": (ml_dtypes.float8_e4m3fn, 7), "e5m2": (ml_dtypes.float8_e5m2, 14)}[fmt]
    v = np.moveaxis(np.asarray(x, np.float32).astype(ml_dtypes.bfloat16).astype(np.float64), axis, -1)
    blocks = v.reshape(v.shape[:-1] + (-1, 32))
    amax = np.abs(blocks).max(-1, keepdims=True)
    byte = np.maximum(np.where(amax > 0, np.frexp(amax)[1] - 1 + 127, 0) - down, 1)
    scale = np.exp2(byte - 127.0)
    codes = (blocks / scale).astype(np.float32).astype(dtype).astype(np.float64)
    return np.moveaxis((codes * scale).reshape(v.shape), -1, axis)


WIDE = False


def mx_kscale(k):
    if not WIDE:
        return np.ones(k)
    levels = np.array([10, -10, 5, -5, 0])
    if k % 512:
        return np.exp2(np.random.permutation(np.resize(levels, k // 32))).repeat(32)
    a = np.empty((k // 512, 16))
    for p in range(k // 512):
        a[p, :8] = np.random.permutation(np.resize(levels, 8))
        for g in range(8):
            far = levels[np.abs(levels - a[p, g]) >= 10]
            a[p, g + 8] = far[np.random.randint(len(far))]
    return np.exp2(a.ravel()).repeat(32)


def f64(x):
    return np.asarray(x).astype(np.float64)


def striped(idx):
    return np.tile(idx.reshape(-1, 16).T, (8, 1)).astype(np.uint16)


def unstriped(offs):
    return offs[:16].T.reshape(-1).astype(np.int64)


def pack_weight(w):
    k, n = w.shape
    w = f64(np.asarray(w, np.float32).astype(ml_dtypes.bfloat16)).reshape(k // 32, 32, n)
    amax = np.abs(w).max(1)
    byte = np.clip(np.where(amax > 0, np.frexp(amax)[1] - 1 + 127 - 7, 1), 1, 254)
    scaled = (w * np.exp2(127.0 - byte)[:, None, :]).reshape(k, n).astype(np.float32)
    words = np.ascontiguousarray(scaled.reshape(k // 512, 128, 4, n).transpose(0, 1, 3, 2)).astype(ml_dtypes.float8_e4m3fn).view(np.uint8)
    return words, np.ascontiguousarray(byte.astype(np.uint8).reshape(k // 512, 16, n))


def unpack_weight(words, scales):
    g, p, n, _ = words.shape
    vals = np.ascontiguousarray(words).view(ml_dtypes.float8_e4m3fn).astype(np.float64) * np.repeat(np.exp2(scales.astype(np.float64) - 127.0), 8, axis=1)[..., None]
    return vals.transpose(0, 1, 3, 2).reshape(g * 512, n)


K, T, E, C, N = 512, 640, 5, 256, 384
M = 512


def by_expert(wq, xq):
    return np.concatenate([wq[e].T @ xq[:, e * C:(e + 1) * C] for e in range(E)], axis=1)


def setup_inputs():
    n = np.random.standard_normal
    s = mx_kscale(K)[:, None]
    first = np.random.permutation(np.repeat(np.arange(E), T // E))
    second = (first + 1 + np.random.permutation(np.repeat(np.arange(E - 1), -(-T // (E - 1)))[:T])) % E
    while np.bincount(second, minlength=E).max() != T // E:
        load = np.bincount(second, minlength=E); hi, lo = int(load.argmax()), int(load.argmin())
        t = np.flatnonzero((second == hi) & (first != lo))[0]; second[t] = lo
    slot_token = np.empty(E * C, np.int64); pos = np.empty((2, T), np.int64); fill = np.zeros(E, np.int64)
    place = np.stack([np.random.permutation(C) for _ in range(E)])
    for r, deal in enumerate((first, second)):
        for t in np.random.permutation(T):
            e = deal[t]; j = e * C + place[e, fill[e]]; fill[e] += 1; slot_token[j] = t; pos[r, t] = j
    g = np.random.uniform(0.2, 0.8, T)
    packed = [pack_weight(m) for m in n((E, K, N)) / np.sqrt(K) / s[None]]
    r = mx_kscale(M)[:, None]
    return {
        "uT": (n((M, T)) * r).astype(np.float32),
        "wu": (n((M, K)) / np.sqrt(M) / r * s.T).astype(np.float32),
        "w_words": np.stack([m[0] for m in packed]),
        "w_scales": np.stack([m[1] for m in packed]),
        "gate": np.stack([np.tile(g, (N, 1)), np.tile(1.0 - g, (N, 1))]).astype(np.float32),
        "offs": striped(slot_token),
        "pos1": striped(pos[0]),
        "pos2": striped(pos[1]),
    }


def reference(uT, wu, w_words, w_scales, gate, offs, pos1, pos2):
    idx = unstriped(offs)
    w = np.stack([unpack_weight(w_words[e], w_scales[e]) for e in range(E)])
    x = mxq(f64(wu), 0, "e4m3").T @ mxq(f64(uT), 0, "e4m3")
    xq = mxq(x[:, idx], 0, "e4m3")
    y = by_expert(w, xq)
    return f64(gate[0]) * y[:, unstriped(pos1)] + f64(gate[1]) * y[:, unstriped(pos2)]

@@ -1,0 +1,242 @@
+from contextlib import ExitStack
+
+import concourse.mybir as mybir
+
+K, T, E, C, N, M = 512, 640, 5, 256, 384, 512
+S = E * C
+FLOPS = 2 * M * K * T + 2 * K * N * S
+
+F32 = mybir.dt.float32
+BF16 = mybir.dt.bfloat16
+I32 = mybir.dt.int32
+U32 = mybir.dt.uint32
+U16 = mybir.dt.uint16
+U8 = mybir.dt.uint8
+FP8X4 = mybir.dt.float8_e4m3fn_x4
+MULT = mybir.AluOpType.mult
+ADD = mybir.AluOpType.add
+
+P = 128
+WINDOW = 704
+TOKEN_CHUNKS = ((0, 256), (256, 256), (512, 128))
+SLOT_CHUNKS = ((0, 512), (512, 512), (1024, 128), (1152, 128))
+
+
+def tile_moe_prv_lin_none_kernel(tc, uT, wu, w_words, w_scales, gate, offs, pos1, pos2, out):
+    nc = tc.nc
+    with ExitStack() as ctx:
+        keep = ctx.enter_context(tc.tile_pool(name="keep", bufs=1))
+        psum = ctx.enter_context(tc.psum_pool(name="psum", bufs=1))
+
+        def bank(b, name):
+            return psum.tile([P, 512], F32, name=name, tag="bank%d" % b)
+
+        wu_rows = wu.rearrange("(p j) c -> p j c", j=4)
+        u_rows = uT.rearrange("(p j) t -> p j t", j=4)
+        wu_raw = [keep.tile([P, 4, 256], F32, name="wu_raw%d" % h) for h in range(2)]
+        for h in range(2):
+            nc.sync.dma_start(out=wu_raw[h][:], in_=wu_rows[:, :, 256 * h : 256 * (h + 1)])
+        u_raw = [keep.tile([P, 4, w], F32, name="u_raw%d" % c) for c, (t0, w) in enumerate(TOKEN_CHUNKS)]
+        for c, (t0, w) in enumerate(TOKEN_CHUNKS):
+            nc.sync.dma_start(out=u_raw[c][:], in_=u_rows[:, :, t0 : t0 + w])
+        offs_sb = keep.tile([P, S // 16], U16, name="offs_sb")
+        nc.sync.dma_start(offs_sb[:], offs)
+
+        w_plane = keep.tile([P, E, N], U8, name="w_plane", align_bytes=64)
+        nc.gpsimd.memset(w_plane[:].bitcast(I32), 0)
+        zeros = keep.tile([P, 2 * (WINDOW - T)], F32, name="zeros")
+        nc.gpsimd.memset(zeros[:], 0.0)
+        for q in range(4):
+            nc.sync.dma_start(
+                out=w_plane[32 * q : 32 * q + 4, :, :].bitcast(I32),
+                in_=w_scales[:, 0, 4 * q : 4 * q + 4, :].rearrange("e q n -> q e n").bitcast(I32),
+            )
+        w_codes = keep.tile([P, E, N], U32, name="w_codes", align_bytes=64)
+        nc.sync.dma_start(
+            out=w_codes[:].bitcast(I32),
+            in_=w_words[:, 0, :, :, :].rearrange("e p n r -> p e (n r)").bitcast(I32),
+        )
+        pos1_sb = keep.tile([P, T // 16], U16, name="pos1_sb")
+        nc.sync.dma_start(pos1_sb[:], pos1)
+        pos2_sb = keep.tile([P, T // 16], U16, name="pos2_sb")
+        nc.sync.dma_start(pos2_sb[:], pos2)
+        gate_sb = [keep.tile([P, 2, T], F32, name="gate%d" % i) for i in range(3)]
+        for i in range(3):
+            nc.sync.dma_start(out=gate_sb[i][:], in_=gate[:, P * i : P * (i + 1), :].rearrange("r p t -> p r t"))
+
+        x_pairs = [keep.tile([P, WINDOW, 2], BF16, name="x_pairs%d" % u) for u in range(2)]
+        for u in range(2):
+            nc.scalar.copy(out=x_pairs[u][:, T:WINDOW, :].rearrange("p t e -> p (t e)"), in_=zeros[:])
+
+        wu_bf = [keep.tile([P, 4, 64, 4], BF16, name="wu_bf%d" % h, align_bytes=64) for h in range(2)]
+        wu_codes = keep.tile([P, 4, P], U32, name="wu_codes", align_bytes=64)
+        wu_plane = keep.tile([P, 4, P], U8, name="wu_plane", align_bytes=64)
+
+        def wu_views(h):
+            return dict(out=wu_bf[h][:].rearrange("p t m j -> p m j t"), in_=wu_raw[h][:].rearrange("p j (m t) -> p m j t", t=4))
+
+        def wu_quantize(h):
+            for t in range(4):
+                nc.vector.quantize_mx(
+                    out=wu_codes[:, t, 64 * h : 64 * (h + 1)].bitcast(FP8X4),
+                    scales=wu_plane[:, t, 64 * h : 64 * (h + 1)],
+                    in_=wu_bf[h][:, t, :, :].rearrange("p m j -> p (m j)"),
+                )
+
+        u_bf = [keep.tile([P, w, 4], BF16, name="u_bf%d" % c, align_bytes=64) for c, (t0, w) in enumerate(TOKEN_CHUNKS)]
+        u_codes = [keep.tile([P, w], U32, name="u_codes%d" % c, align_bytes=64) for c, (t0, w) in enumerate(TOKEN_CHUNKS)]
+        u_plane = [keep.tile([P, w], U8, name="u_plane%d" % c, align_bytes=64) for c, (t0, w) in enumerate(TOKEN_CHUNKS)]
+
+        def u_views(c, a, b):
+            return dict(
+                out=u_bf[c][:, a:b, :].rearrange("p (g i) j -> p g j i", i=4),
+                in_=u_raw[c][:, :, a:b].rearrange("p j (g i) -> p g j i", i=4),
+            )
+
+        def u_quantize(c):
+            nc.vector.quantize_mx(out=u_codes[c][:].bitcast(FP8X4), scales=u_plane[c][:], in_=u_bf[c][:].rearrange("p w j -> p (w j)"))
+
+        x_banks = {}
+
+        def project(c):
+            w = TOKEN_CHUNKS[c][1]
+            for u in range(2):
+                x_banks[c, u] = bank(2 * c + u, "x_bank%d%d" % (c, u))
+                for e in range(2):
+                    t = 2 * u + e
+                    nc.tensor.matmul_mx(
+                        out=x_banks[c, u][:, e * w : (e + 1) * w],
+                        lhsT=wu_codes[:, t, :].bitcast(FP8X4),
+                        lhsT_scale=wu_plane[:, t, :],
+                        rhs=u_codes[c][:].bitcast(FP8X4),
+                        rhs_scale=u_plane[c][:],
+                        start=True,
+                        stop=True,
+                    )
+
+        def x_views(c, u):
+            t0, w = TOKEN_CHUNKS[c]
+            return dict(out=x_pairs[u][:, t0 : t0 + w, :], in_=x_banks[c, u][:, 0 : 2 * w].rearrange("p (e t) -> p t e", e=2))
+
+        nc.scalar.copy(**wu_views(0))
+        nc.vector.tensor_copy(**wu_views(1))
+        wu_quantize(0)
+        wu_quantize(1)
+        nc.vector.tensor_copy(**u_views(0, 0, 256))
+        u_quantize(0)
+        project(0)
+        nc.vector.tensor_copy(**u_views(1, 0, 128))
+        nc.scalar.copy(**u_views(1, 128, 256))
+        nc.scalar.copy(**x_views(0, 0))
+        nc.scalar.copy(**x_views(0, 1))
+        nc.vector.tensor_copy(**u_views(2, 0, 128))
+        u_quantize(1)
+        u_quantize(2)
+        project(1)
+        project(2)
+        nc.scalar.copy(**x_views(1, 0))
+        nc.vector.tensor_copy(**x_views(1, 1))
+        nc.scalar.copy(**x_views(2, 0))
+        nc.vector.tensor_copy(**x_views(2, 1))
+
+        xs_bf = [keep.tile([P, n, 4], BF16, name="xs_bf%d" % c, align_bytes=64) for c, (s0, n) in enumerate(SLOT_CHUNKS)]
+        xs_codes = keep.tile([P, S], U32, name="xs_codes", align_bytes=64)
+        xs_plane = keep.tile([P, S], U8, name="xs_plane", align_bytes=64)
+
+        def gather_x(c, u):
+            s0, n = SLOT_CHUNKS[c]
+            words = xs_bf[c][:].rearrange("p s j -> p (s j)").bitcast(U32).rearrange("p (s u) -> p s u", u=2)
+            window = x_pairs[u][:].rearrange("p t e -> p (t e)").bitcast(U32)
+            nc.vector.tensor_copy(words[:, :, u], window.indirect(offs_sb[:, s0 // 16 : (s0 + n) // 16]))
+
+        def xs_quantize(c):
+            s0, n = SLOT_CHUNKS[c]
+            nc.vector.quantize_mx(
+                out=xs_codes[:, s0 : s0 + n].bitcast(FP8X4),
+                scales=xs_plane[:, s0 : s0 + n],
+                in_=xs_bf[c][:].rearrange("p s j -> p (s j)"),
+            )
+
+        y_sb = [keep.tile([P, S], F32, name="y_sb%d" % i) for i in range(3)]
+        y_banks = {}
+        for i in range(3):
+            for c in range(2):
+                y_banks[i, c] = (bank((6 + 2 * i + c) % 8, "y_bank%d%d" % (i, c)), 0)
+        first = bank(4, "y_last_first")
+        rest = bank(5, "y_last_rest")
+        y_banks[0, 2] = (first, 0)
+        y_banks[0, 3] = (first, 128)
+        for i in (1, 2):
+            for c in (2, 3):
+                y_banks[i, c] = (rest, 256 * (i - 1) + 128 * (c - 2))
+
+        def experts(i, c):
+            s0, n = SLOT_CHUNKS[c]
+            tile_, col = y_banks[i, c]
+            step = min(n, C)
+            for a in range(0, n, step):
+                e = (s0 + a) // C
+                nc.tensor.matmul_mx(
+                    out=tile_[:, col + a : col + a + step],
+                    lhsT=w_codes[:, e, P * i : P * (i + 1)].bitcast(FP8X4),
+                    lhsT_scale=w_plane[:, e, P * i : P * (i + 1)],
+                    rhs=xs_codes[:, s0 + a : s0 + a + step].bitcast(FP8X4),
+                    rhs_scale=xs_plane[:, s0 + a : s0 + a + step],
+                    start=True,
+                    stop=True,
+                )
+
+        def y_out(i, c, chunks=1):
+            s0, n = SLOT_CHUNKS[c]
+            tile_, col = y_banks[i, c]
+            nc.scalar.copy(out=y_sb[i][:, s0 : s0 + n * chunks], in_=tile_[:, col : col + n * chunks])
+
+        gather_x(0, 0)
+        gather_x(0, 1)
+        gather_x(1, 0)
+        xs_quantize(0)
+        gather_x(1, 1)
+        gather_x(2, 0)
+        xs_quantize(1)
+        gather_x(2, 1)
+        gather_x(3, 0)
+        gather_x(3, 1)
+        xs_quantize(2)
+        xs_quantize(3)
+        for c in range(4):
+            experts(0, c)
+        y_out(0, 0)
+        y_out(0, 1)
+        y_out(0, 2, 2)
+        for i in (1, 2):
+            for c in range(4):
+                experts(i, c)
+        for i in (1, 2):
+            y_out(i, 0)
+            y_out(i, 1)
+            y_out(i, 2, 2)
+
+        a_sb = [keep.tile([P, T], F32, name="a_sb%d" % i) for i in range(3)]
+        b_sb = [keep.tile([P, T], F32, name="b_sb%d" % i) for i in range(3)]
+        o_sb = [keep.tile([P, T], F32, name="o_sb%d" % i) for i in range(3)]
+
+        def fetch(i, r, t0, t1):
+            dst = (a_sb, b_sb)[r][i]
+            lst = (pos1_sb, pos2_sb)[r]
+            nc.vector.tensor_tensor(dst[:, t0:t1], y_sb[i][:].indirect(lst[:, t0 // 16 : t1 // 16]), gate_sb[i][:, r, t0:t1], MULT)
+
+        def finish(i, t0, t1):
+            nc.vector.tensor_tensor(o_sb[i][:, t0:t1], a_sb[i][:, t0:t1], b_sb[i][:, t0:t1], ADD)
+            nc.sync.dma_start(out=out[P * i : P * (i + 1), t0:t1], in_=o_sb[i][:, t0:t1])
+
+        fetch(0, 0, 0, T)
+        fetch(0, 1, 0, T)
+        fetch(1, 0, 0, T)
+        finish(0, 0, T)
+        fetch(1, 1, 0, T)
+        fetch(2, 0, 0, T)
+        finish(1, 0, T)
+        fetch(2, 1, 0, 384)
+        fetch(2, 1, 384, T)
+        finish(2, 0, 384)
+        finish(2, 384, T)

@@ -1,6 +1,7 @@
 from contextlib import ExitStack
 
 import concourse.mybir as mybir
+from concourse.masks import make_identity
 
 K, T, E, C, N, M = 512, 640, 5, 256, 384, 512
 S = E * C
@@ -19,7 +20,7 @@ ADD = mybir.AluOpType.add
 P = 128
 WINDOW = 704
 TOKEN_CHUNKS = ((0, 256), (256, 256), (512, 128))
-SLOT_CHUNKS = ((0, 512), (512, 512), (1024, 128), (1152, 128))
+SLOT_CHUNKS = ((0, 512), (512, 256), (768, 256), (1024, 256))
 
 
 def tile_moe_prv_lin_none_kernel(tc, uT, wu, w_words, w_scales, gate, offs, pos1, pos2, out):
@@ -46,6 +47,8 @@ def tile_moe_prv_lin_none_kernel(tc, uT, wu, w_words, w_scales, gate, offs, pos1
         nc.gpsimd.memset(w_plane[:].bitcast(I32), 0)
         zeros = keep.tile([P, 2 * (WINDOW - T)], F32, name="zeros")
         nc.gpsimd.memset(zeros[:], 0.0)
+        ident = keep.tile([P, P], F32, name="ident")
+        make_identity(nc, ident[:])
         for q in range(4):
             nc.sync.dma_start(
                 out=w_plane[32 * q : 32 * q + 4, :, :].bitcast(I32),
@@ -139,22 +142,26 @@ def tile_moe_prv_lin_none_kernel(tc, uT, wu, w_words, w_scales, gate, offs, pos1
         nc.scalar.copy(**x_views(2, 0))
         nc.vector.tensor_copy(**x_views(2, 1))
 
+        xs_planes = [keep.tile([P, 2, n], U32, name="xs_planes%d" % c) for c, (s0, n) in enumerate(SLOT_CHUNKS)]
         xs_bf = [keep.tile([P, n, 4], BF16, name="xs_bf%d" % c, align_bytes=64) for c, (s0, n) in enumerate(SLOT_CHUNKS)]
         xs_codes = keep.tile([P, S], U32, name="xs_codes", align_bytes=64)
         xs_plane = keep.tile([P, S], U8, name="xs_plane", align_bytes=64)
 
         def gather_x(c, u):
             s0, n = SLOT_CHUNKS[c]
-            words = xs_bf[c][:].rearrange("p s j -> p (s j)").bitcast(U32).rearrange("p (s u) -> p s u", u=2)
             window = x_pairs[u][:].rearrange("p t e -> p (t e)").bitcast(U32)
-            nc.vector.tensor_copy(words[:, :, u], window.indirect(offs_sb[:, s0 // 16 : (s0 + n) // 16]))
+            nc.vector.tensor_copy(xs_planes[c][:, u, :], window.indirect(offs_sb[:, s0 // 16 : (s0 + n) // 16]))
 
-        def xs_quantize(c):
+        def xs_views(c, a, b, dtype):
+            words = xs_bf[c][:].rearrange("p s j -> p (s j)").bitcast(dtype).rearrange("p (s u) -> p s u", u=2)
+            return dict(out=words[:, a:b, :], in_=xs_planes[c][:].bitcast(dtype).rearrange("p u s -> p s u")[:, a:b, :])
+
+        def xs_quantize(c, a, b):
             s0, n = SLOT_CHUNKS[c]
             nc.vector.quantize_mx(
-                out=xs_codes[:, s0 : s0 + n].bitcast(FP8X4),
-                scales=xs_plane[:, s0 : s0 + n],
-                in_=xs_bf[c][:].rearrange("p s j -> p (s j)"),
+                out=xs_codes[:, s0 + a : s0 + b].bitcast(FP8X4),
+                scales=xs_plane[:, s0 + a : s0 + b],
+                in_=xs_bf[c][:, a:b, :].rearrange("p s j -> p (s j)"),
             )
 
         y_sb = [keep.tile([P, S], F32, name="y_sb%d" % i) for i in range(3)]
@@ -165,78 +172,109 @@ def tile_moe_prv_lin_none_kernel(tc, uT, wu, w_words, w_scales, gate, offs, pos1
         first = bank(4, "y_last_first")
         rest = bank(5, "y_last_rest")
         y_banks[0, 2] = (first, 0)
-        y_banks[0, 3] = (first, 128)
-        for i in (1, 2):
-            for c in (2, 3):
-                y_banks[i, c] = (rest, 256 * (i - 1) + 128 * (c - 2))
+        y_banks[1, 2] = (rest, 0)
+        y_banks[2, 2] = (rest, 256)
 
-        def experts(i, c):
-            s0, n = SLOT_CHUNKS[c]
-            tile_, col = y_banks[i, c]
-            step = min(n, C)
-            for a in range(0, n, step):
-                e = (s0 + a) // C
-                nc.tensor.matmul_mx(
-                    out=tile_[:, col + a : col + a + step],
-                    lhsT=w_codes[:, e, P * i : P * (i + 1)].bitcast(FP8X4),
-                    lhsT_scale=w_plane[:, e, P * i : P * (i + 1)],
-                    rhs=xs_codes[:, s0 + a : s0 + a + step].bitcast(FP8X4),
-                    rhs_scale=xs_plane[:, s0 + a : s0 + a + step],
-                    start=True,
-                    stop=True,
-                )
+        def expert(i, s0, n):
+            tile_, col = y_banks[i, s0 // 512]
+            col += s0 % 512
+            e = s0 // C
+            nc.tensor.matmul_mx(
+                out=tile_[:, col : col + n],
+                lhsT=w_codes[:, e, P * i : P * (i + 1)].bitcast(FP8X4),
+                lhsT_scale=w_plane[:, e, P * i : P * (i + 1)],
+                rhs=xs_codes[:, s0 : s0 + n].bitcast(FP8X4),
+                rhs_scale=xs_plane[:, s0 : s0 + n],
+                start=True,
+                stop=True,
+            )
 
-        def y_out(i, c, chunks=1):
-            s0, n = SLOT_CHUNKS[c]
-            tile_, col = y_banks[i, c]
-            nc.scalar.copy(out=y_sb[i][:, s0 : s0 + n * chunks], in_=tile_[:, col : col + n * chunks])
+        def y_out(i, s0, n):
+            tile_, col = y_banks[i, s0 // 512]
+            col += s0 % 512
+            nc.scalar.copy(out=y_sb[i][:, s0 : s0 + n], in_=tile_[:, col : col + n])
 
         gather_x(0, 0)
         gather_x(0, 1)
+        nc.scalar.copy(**xs_views(0, 0, 512, F32))
         gather_x(1, 0)
-        xs_quantize(0)
         gather_x(1, 1)
+        nc.scalar.copy(**xs_views(1, 0, 256, F32))
+        xs_quantize(0, 0, 512)
         gather_x(2, 0)
-        xs_quantize(1)
         gather_x(2, 1)
+        nc.scalar.copy(**xs_views(2, 0, 256, F32))
+        xs_quantize(1, 0, 256)
         gather_x(3, 0)
         gather_x(3, 1)
-        xs_quantize(2)
-        xs_quantize(3)
-        for c in range(4):
-            experts(0, c)
-        y_out(0, 0)
-        y_out(0, 1)
-        y_out(0, 2, 2)
+        xs_quantize(2, 0, 256)
+        nc.vector.tensor_copy(**xs_views(3, 0, 128, I32))
+        nc.vector.tensor_copy(**xs_views(3, 128, 256, I32))
+        xs_quantize(3, 0, 128)
+        xs_quantize(3, 128, 256)
+        pieces = [(0, 256), (256, 256), (512, 256), (768, 256), (1024, 128), (1152, 128)]
+        for s0, n in pieces:
+            expert(0, s0, n)
+        y_out(0, 0, 512)
+        y_out(0, 512, 512)
+        y_out(0, 1024, 256)
         for i in (1, 2):
-            for c in range(4):
-                experts(i, c)
+            for e in range(E):
+                expert(i, C * e, C)
         for i in (1, 2):
-            y_out(i, 0)
-            y_out(i, 1)
-            y_out(i, 2, 2)
+            y_out(i, 0, 512)
+            y_out(i, 512, 512)
+            y_out(i, 1024, 256)
 
-        a_sb = [keep.tile([P, T], F32, name="a_sb%d" % i) for i in range(3)]
-        b_sb = [keep.tile([P, T], F32, name="b_sb%d" % i) for i in range(3)]
+        terms = [[keep.tile([P, T], F32, name="term%d%d" % (i, r)) for r in range(2)] for i in range(3)]
         o_sb = [keep.tile([P, T], F32, name="o_sb%d" % i) for i in range(3)]
+        turned = [keep.tile([P, T], F32, name="turned%d" % i) for i in range(2)]
+        lists = (pos1_sb, pos2_sb)
+        halves = ((0, 384), (384, T))
 
         def fetch(i, r, t0, t1):
-            dst = (a_sb, b_sb)[r][i]
-            lst = (pos1_sb, pos2_sb)[r]
-            nc.vector.tensor_tensor(dst[:, t0:t1], y_sb[i][:].indirect(lst[:, t0 // 16 : t1 // 16]), gate_sb[i][:, r, t0:t1], MULT)
+            nc.vector.tensor_tensor(
+                terms[i][r][:, t0:t1], y_sb[i][:].indirect(lists[r][:, t0 // 16 : t1 // 16]), gate_sb[i][:, r, t0:t1], MULT
+            )
 
-        def finish(i, t0, t1):
-            nc.vector.tensor_tensor(o_sb[i][:, t0:t1], a_sb[i][:, t0:t1], b_sb[i][:, t0:t1], ADD)
+        def store(i, t0, t1):
             nc.sync.dma_start(out=out[P * i : P * (i + 1), t0:t1], in_=o_sb[i][:, t0:t1])
+
+        def add_on_vector(i, t0, t1):
+            nc.vector.tensor_tensor(o_sb[i][:, t0:t1], terms[i][0][:, t0:t1], terms[i][1][:, t0:t1], ADD)
+            store(i, t0, t1)
+
+        def add_in_psum(i, banks):
+            there = [bank(banks[h], "there%d%d" % (i, h)) for h in range(2)]
+            back = [bank(banks[2 + h], "back%d%d" % (i, h)) for h in range(2)]
+            for r in range(2):
+                for h, (t0, t1) in enumerate(halves):
+                    for t in range(t0, t1, P):
+                        nc.tensor.matmul(
+                            there[h][:, t - t0 : t - t0 + P],
+                            terms[i][r][:, t : t + P],
+                            ident[:],
+                            start=(r == 0 and t == t0),
+                            stop=(r == 1 and t == t1 - P),
+                            is_transpose=True,
+                        )
+            for h, (t0, t1) in enumerate(halves):
+                nc.scalar.copy(out=turned[i][:, t0:t1], in_=there[h][:, 0 : t1 - t0])
+            for h, (t0, t1) in enumerate(halves):
+                for t in range(t0, t1, P):
+                    nc.tensor.transpose(back[h][:, t - t0 : t - t0 + P], turned[i][:, t : t + P], ident[:])
+            for h, (t0, t1) in enumerate(halves):
+                nc.scalar.copy(out=o_sb[i][:, t0:t1], in_=back[h][:, 0 : t1 - t0])
+            store(i, 0, T)
 
         fetch(0, 0, 0, T)
         fetch(0, 1, 0, T)
+        add_in_psum(0, (6, 7, 4, 0))
         fetch(1, 0, 0, T)
-        finish(0, 0, T)
         fetch(1, 1, 0, T)
+        add_in_psum(1, (1, 2, 3, 5))
         fetch(2, 0, 0, T)
-        finish(1, 0, T)
         fetch(2, 1, 0, 384)
         fetch(2, 1, 384, T)
-        finish(2, 0, 384)
-        finish(2, 384, T)
+        add_on_vector(2, 0, 384)
+        add_on_vector(2, 384, T)

@@ -18,9 +18,10 @@ MULT = mybir.AluOpType.mult
 ADD = mybir.AluOpType.add
 
 P = 128
-WINDOW = 704
-TOKEN_CHUNKS = ((0, 256), (256, 256), (512, 128))
-SLOT_CHUNKS = ((0, 512), (512, 256), (768, 256), (1024, 256))
+TOKEN_LOADS = ((0, 256), (256, 256), (512, 128))
+TOKEN_GROUPS = ((0, 256), (256, 128), (384, 128), (512, 128))
+SLOT_CHUNKS = ((0, 448), (448, 448), (896, 384))
+SLOT_GROUPS = ((0, 256), (256, 256), (512, 256), (768, 256), (1024, 128), (1152, 128))
 
 
 def tile_moe_prv_lin_none_kernel(tc, uT, wu, w_words, w_scales, gate, offs, pos1, pos2, out):
@@ -37,16 +38,14 @@ def tile_moe_prv_lin_none_kernel(tc, uT, wu, w_words, w_scales, gate, offs, pos1
         wu_raw = [keep.tile([P, 4, 256], F32, name="wu_raw%d" % h) for h in range(2)]
         for h in range(2):
             nc.sync.dma_start(out=wu_raw[h][:], in_=wu_rows[:, :, 256 * h : 256 * (h + 1)])
-        u_raw = [keep.tile([P, 4, w], F32, name="u_raw%d" % c) for c, (t0, w) in enumerate(TOKEN_CHUNKS)]
-        for c, (t0, w) in enumerate(TOKEN_CHUNKS):
+        u_raw = [keep.tile([P, 4, w], F32, name="u_raw%d" % c) for c, (t0, w) in enumerate(TOKEN_LOADS)]
+        for c, (t0, w) in enumerate(TOKEN_LOADS):
             nc.sync.dma_start(out=u_raw[c][:], in_=u_rows[:, :, t0 : t0 + w])
         offs_sb = keep.tile([P, S // 16], U16, name="offs_sb")
         nc.sync.dma_start(offs_sb[:], offs)
 
         w_plane = keep.tile([P, E, N], U8, name="w_plane", align_bytes=64)
         nc.gpsimd.memset(w_plane[:].bitcast(I32), 0)
-        zeros = keep.tile([P, 2 * (WINDOW - T)], F32, name="zeros")
-        nc.gpsimd.memset(zeros[:], 0.0)
         ident = keep.tile([P, P], F32, name="ident")
         make_identity(nc, ident[:])
         for q in range(4):
@@ -67,83 +66,82 @@ def tile_moe_prv_lin_none_kernel(tc, uT, wu, w_words, w_scales, gate, offs, pos1
         for i in range(3):
             nc.sync.dma_start(out=gate_sb[i][:], in_=gate[:, P * i : P * (i + 1), :].rearrange("r p t -> p r t"))
 
-        x_pairs = [keep.tile([P, WINDOW, 2], BF16, name="x_pairs%d" % u) for u in range(2)]
-        for u in range(2):
-            nc.scalar.copy(out=x_pairs[u][:, T:WINDOW, :].rearrange("p t e -> p (t e)"), in_=zeros[:])
+        x_pairs = [keep.tile([P, T, 2], BF16, name="x_pairs%d" % u) for u in range(2)]
 
-        wu_bf = [keep.tile([P, 4, 64, 4], BF16, name="wu_bf%d" % h, align_bytes=64) for h in range(2)]
+        wu_bf = keep.tile([P, 4, P, 4], BF16, name="wu_bf", align_bytes=64)
         wu_codes = keep.tile([P, 4, P], U32, name="wu_codes", align_bytes=64)
         wu_plane = keep.tile([P, 4, P], U8, name="wu_plane", align_bytes=64)
 
-        def wu_views(h):
-            return dict(out=wu_bf[h][:].rearrange("p t m j -> p m j t"), in_=wu_raw[h][:].rearrange("p j (m t) -> p m j t", t=4))
+        def wu_views(h, a, b):
+            return dict(
+                out=wu_bf[:].rearrange("p t m j -> p m j t")[:, 64 * h + a : 64 * h + b, :, :],
+                in_=wu_raw[h][:].rearrange("p j (m t) -> p m j t", t=4)[:, a:b, :, :],
+            )
 
-        def wu_quantize(h):
-            for t in range(4):
-                nc.vector.quantize_mx(
-                    out=wu_codes[:, t, 64 * h : 64 * (h + 1)].bitcast(FP8X4),
-                    scales=wu_plane[:, t, 64 * h : 64 * (h + 1)],
-                    in_=wu_bf[h][:, t, :, :].rearrange("p m j -> p (m j)"),
-                )
+        def wu_quantize(u):
+            nc.vector.quantize_mx(
+                out=wu_codes[:, 2 * u : 2 * u + 2, :].rearrange("p t m -> p (t m)").bitcast(FP8X4),
+                scales=wu_plane[:, 2 * u : 2 * u + 2, :].rearrange("p t m -> p (t m)"),
+                in_=wu_bf[:, 2 * u : 2 * u + 2, :, :].rearrange("p t m j -> p (t m j)"),
+            )
 
-        u_bf = [keep.tile([P, w, 4], BF16, name="u_bf%d" % c, align_bytes=64) for c, (t0, w) in enumerate(TOKEN_CHUNKS)]
-        u_codes = [keep.tile([P, w], U32, name="u_codes%d" % c, align_bytes=64) for c, (t0, w) in enumerate(TOKEN_CHUNKS)]
-        u_plane = [keep.tile([P, w], U8, name="u_plane%d" % c, align_bytes=64) for c, (t0, w) in enumerate(TOKEN_CHUNKS)]
+        u_bf = [keep.tile([P, w, 4], BF16, name="u_bf%d" % c, align_bytes=64) for c, (t0, w) in enumerate(TOKEN_GROUPS)]
+        u_codes = keep.tile([P, T], U32, name="u_codes", align_bytes=64)
+        u_plane = keep.tile([P, T], U8, name="u_plane", align_bytes=64)
 
         def u_views(c, a, b):
+            load, lo = divmod(TOKEN_GROUPS[c][0], 256)
             return dict(
                 out=u_bf[c][:, a:b, :].rearrange("p (g i) j -> p g j i", i=4),
-                in_=u_raw[c][:, :, a:b].rearrange("p j (g i) -> p g j i", i=4),
+                in_=u_raw[load][:, :, lo + a : lo + b].rearrange("p j (g i) -> p g j i", i=4),
             )
 
         def u_quantize(c):
-            nc.vector.quantize_mx(out=u_codes[c][:].bitcast(FP8X4), scales=u_plane[c][:], in_=u_bf[c][:].rearrange("p w j -> p (w j)"))
+            t0, w = TOKEN_GROUPS[c]
+            nc.vector.quantize_mx(
+                out=u_codes[:, t0 : t0 + w].bitcast(FP8X4),
+                scales=u_plane[:, t0 : t0 + w],
+                in_=u_bf[c][:].rearrange("p w j -> p (w j)"),
+            )
 
-        x_banks = {}
+        def project(u, t0, w, sums):
+            for e in range(2):
+                t = 2 * u + e
+                nc.tensor.matmul_mx(
+                    out=sums[:, e * w : (e + 1) * w],
+                    lhsT=wu_codes[:, t, :].bitcast(FP8X4),
+                    lhsT_scale=wu_plane[:, t, :],
+                    rhs=u_codes[:, t0 : t0 + w].bitcast(FP8X4),
+                    rhs_scale=u_plane[:, t0 : t0 + w],
+                    start=True,
+                    stop=True,
+                )
+            return dict(out=x_pairs[u][:, t0 : t0 + w, :], in_=sums.rearrange("p (e t) -> p t e", e=2))
 
-        def project(c):
-            w = TOKEN_CHUNKS[c][1]
-            for u in range(2):
-                x_banks[c, u] = bank(2 * c + u, "x_bank%d%d" % (c, u))
-                for e in range(2):
-                    t = 2 * u + e
-                    nc.tensor.matmul_mx(
-                        out=x_banks[c, u][:, e * w : (e + 1) * w],
-                        lhsT=wu_codes[:, t, :].bitcast(FP8X4),
-                        lhsT_scale=wu_plane[:, t, :],
-                        rhs=u_codes[c][:].bitcast(FP8X4),
-                        rhs_scale=u_plane[c][:],
-                        start=True,
-                        stop=True,
-                    )
-
-        def x_views(c, u):
-            t0, w = TOKEN_CHUNKS[c]
-            return dict(out=x_pairs[u][:, t0 : t0 + w, :], in_=x_banks[c, u][:, 0 : 2 * w].rearrange("p (e t) -> p t e", e=2))
-
-        nc.scalar.copy(**wu_views(0))
-        nc.vector.tensor_copy(**wu_views(1))
+        for h in range(2):
+            nc.vector.tensor_copy(**wu_views(h, 0, 40))
+            nc.scalar.copy(**wu_views(h, 40, 64))
         wu_quantize(0)
+        nc.vector.tensor_copy(**u_views(0, 0, 144))
+        nc.scalar.copy(**u_views(0, 144, 256))
         wu_quantize(1)
-        nc.vector.tensor_copy(**u_views(0, 0, 256))
         u_quantize(0)
-        project(0)
+        x_banks = [bank(b, "x_bank%d" % b) for b in range(6)]
+        nc.scalar.copy(**project(0, 0, 256, x_banks[0][:]))
         nc.vector.tensor_copy(**u_views(1, 0, 128))
-        nc.scalar.copy(**u_views(1, 128, 256))
-        nc.scalar.copy(**x_views(0, 0))
-        nc.scalar.copy(**x_views(0, 1))
-        nc.vector.tensor_copy(**u_views(2, 0, 128))
-        u_quantize(1)
-        u_quantize(2)
-        project(1)
-        project(2)
-        nc.scalar.copy(**x_views(1, 0))
-        nc.vector.tensor_copy(**x_views(1, 1))
-        nc.scalar.copy(**x_views(2, 0))
-        nc.vector.tensor_copy(**x_views(2, 1))
+        nc.scalar.copy(**u_views(2, 0, 128))
+        nc.vector.tensor_copy(**u_views(3, 0, 128))
+        for c in (1, 2, 3):
+            u_quantize(c)
+        nc.vector.tensor_copy(**project(0, 256, 128, x_banks[1][:, 0:256]))
+        nc.vector.tensor_copy(**project(0, 384, 128, x_banks[2][:, 0:256]))
+        nc.scalar.copy(**project(0, 512, 128, x_banks[3][:, 0:256]))
+        nc.scalar.copy(**project(1, 0, 256, x_banks[4][:]))
+        nc.scalar.copy(**project(1, 384, 256, x_banks[5][:]))
+        nc.scalar.copy(**project(1, 256, 128, x_banks[3][:, 256:512]))
 
         xs_planes = [keep.tile([P, 2, n], U32, name="xs_planes%d" % c) for c, (s0, n) in enumerate(SLOT_CHUNKS)]
-        xs_bf = [keep.tile([P, n, 4], BF16, name="xs_bf%d" % c, align_bytes=64) for c, (s0, n) in enumerate(SLOT_CHUNKS)]
+        xs_bf = keep.tile([P, S, 4], BF16, name="xs_bf", align_bytes=64)
         xs_codes = keep.tile([P, S], U32, name="xs_codes", align_bytes=64)
         xs_plane = keep.tile([P, S], U8, name="xs_plane", align_bytes=64)
 
@@ -152,35 +150,24 @@ def tile_moe_prv_lin_none_kernel(tc, uT, wu, w_words, w_scales, gate, offs, pos1
             window = x_pairs[u][:].rearrange("p t e -> p (t e)").bitcast(U32)
             nc.vector.tensor_copy(xs_planes[c][:, u, :], window.indirect(offs_sb[:, s0 // 16 : (s0 + n) // 16]))
 
-        def xs_views(c, a, b, dtype):
-            words = xs_bf[c][:].rearrange("p s j -> p (s j)").bitcast(dtype).rearrange("p (s u) -> p s u", u=2)
-            return dict(out=words[:, a:b, :], in_=xs_planes[c][:].bitcast(dtype).rearrange("p u s -> p s u")[:, a:b, :])
-
-        def xs_quantize(c, a, b):
+        def interleave(c):
             s0, n = SLOT_CHUNKS[c]
+            words = xs_bf[:].rearrange("p s j -> p (s j)").bitcast(F32).rearrange("p (s u) -> p s u", u=2)
+            nc.scalar.copy(out=words[:, s0 : s0 + n, :], in_=xs_planes[c][:].bitcast(F32).rearrange("p u s -> p s u"))
+
+        def xs_quantize(s0, n):
             nc.vector.quantize_mx(
-                out=xs_codes[:, s0 + a : s0 + b].bitcast(FP8X4),
-                scales=xs_plane[:, s0 + a : s0 + b],
-                in_=xs_bf[c][:, a:b, :].rearrange("p s j -> p (s j)"),
+                out=xs_codes[:, s0 : s0 + n].bitcast(FP8X4),
+                scales=xs_plane[:, s0 : s0 + n],
+                in_=xs_bf[:, s0 : s0 + n, :].rearrange("p s j -> p (s j)"),
             )
 
         y_sb = [keep.tile([P, S], F32, name="y_sb%d" % i) for i in range(3)]
-        y_banks = {}
-        for i in range(3):
-            for c in range(2):
-                y_banks[i, c] = (bank((6 + 2 * i + c) % 8, "y_bank%d%d" % (i, c)), 0)
-        first = bank(4, "y_last_first")
-        rest = bank(5, "y_last_rest")
-        y_banks[0, 2] = (first, 0)
-        y_banks[1, 2] = (rest, 0)
-        y_banks[2, 2] = (rest, 256)
 
-        def expert(i, s0, n):
-            tile_, col = y_banks[i, s0 // 512]
-            col += s0 % 512
+        def expert(i, s0, n, sums):
             e = s0 // C
             nc.tensor.matmul_mx(
-                out=tile_[:, col : col + n],
+                out=sums,
                 lhsT=w_codes[:, e, P * i : P * (i + 1)].bitcast(FP8X4),
                 lhsT_scale=w_plane[:, e, P * i : P * (i + 1)],
                 rhs=xs_codes[:, s0 : s0 + n].bitcast(FP8X4),
@@ -189,48 +176,39 @@ def tile_moe_prv_lin_none_kernel(tc, uT, wu, w_words, w_scales, gate, offs, pos1
                 stop=True,
             )
 
-        def y_out(i, s0, n):
-            tile_, col = y_banks[i, s0 // 512]
-            col += s0 % 512
-            nc.scalar.copy(out=y_sb[i][:, s0 : s0 + n], in_=tile_[:, col : col + n])
+        def experts(i, s0, n, step, sums):
+            for a in range(0, n, step):
+                expert(i, s0 + a, step, sums[:, a : a + step])
+            return dict(out=y_sb[i][:, s0 : s0 + n], in_=sums)
 
         gather_x(0, 0)
-        gather_x(0, 1)
-        nc.scalar.copy(**xs_views(0, 0, 512, F32))
         gather_x(1, 0)
+        gather_x(0, 1)
+        interleave(0)
         gather_x(1, 1)
-        nc.scalar.copy(**xs_views(1, 0, 256, F32))
-        xs_quantize(0, 0, 512)
+        interleave(1)
         gather_x(2, 0)
         gather_x(2, 1)
-        nc.scalar.copy(**xs_views(2, 0, 256, F32))
-        xs_quantize(1, 0, 256)
-        gather_x(3, 0)
-        gather_x(3, 1)
-        xs_quantize(2, 0, 256)
-        nc.vector.tensor_copy(**xs_views(3, 0, 128, I32))
-        nc.vector.tensor_copy(**xs_views(3, 128, 256, I32))
-        xs_quantize(3, 0, 128)
-        xs_quantize(3, 128, 256)
-        pieces = [(0, 256), (256, 256), (512, 256), (768, 256), (1024, 128), (1152, 128)]
-        for s0, n in pieces:
-            expert(0, s0, n)
-        y_out(0, 0, 512)
-        y_out(0, 512, 512)
-        y_out(0, 1024, 256)
-        for i in (1, 2):
-            for e in range(E):
-                expert(i, C * e, C)
-        for i in (1, 2):
-            y_out(i, 0, 512)
-            y_out(i, 512, 512)
-            y_out(i, 1024, 256)
+        interleave(2)
+        for s0, n in SLOT_GROUPS:
+            xs_quantize(s0, n)
+        y0 = [bank(b, "y0_bank%d" % b) for b in range(5)]
+        nc.scalar.copy(**experts(0, 0, 512, C, y0[0][:]))
+        nc.scalar.copy(**experts(0, 512, C, C, y0[1][:, 0:C]))
+        nc.vector.tensor_copy(**experts(0, 768, C, C, y0[2][:, 0:C]))
+        nc.vector.tensor_copy(**experts(0, 1024, P, P, y0[4][:, 0:P]))
+        nc.vector.tensor_copy(**experts(0, 1152, P, P, y0[3][:, 0:P]))
+        nc.scalar.copy(**experts(1, 0, 512, C, bank(0, "y1_a")[:]))
+        nc.scalar.copy(**experts(1, 512, 512, C, bank(2, "y1_b")[:]))
+        nc.scalar.copy(**experts(1, 1024, C, C, y0[3][:, C:512]))
+        nc.scalar.copy(**experts(2, 1024, C, C, y0[1][:, C:512]))
+        nc.scalar.copy(**experts(2, 0, 512, C, bank(0, "y2_a")[:]))
+        nc.scalar.copy(**experts(2, 512, 512, C, bank(2, "y2_b")[:]))
 
         terms = [[keep.tile([P, T], F32, name="term%d%d" % (i, r)) for r in range(2)] for i in range(3)]
         o_sb = [keep.tile([P, T], F32, name="o_sb%d" % i) for i in range(3)]
         turned = [keep.tile([P, T], F32, name="turned%d" % i) for i in range(2)]
         lists = (pos1_sb, pos2_sb)
-        halves = ((0, 384), (384, T))
 
         def fetch(i, r, t0, t1):
             nc.vector.tensor_tensor(
@@ -244,35 +222,34 @@ def tile_moe_prv_lin_none_kernel(tc, uT, wu, w_words, w_scales, gate, offs, pos1
             nc.vector.tensor_tensor(o_sb[i][:, t0:t1], terms[i][0][:, t0:t1], terms[i][1][:, t0:t1], ADD)
             store(i, t0, t1)
 
-        def add_in_psum(i, banks):
-            there = [bank(banks[h], "there%d%d" % (i, h)) for h in range(2)]
-            back = [bank(banks[2 + h], "back%d%d" % (i, h)) for h in range(2)]
+        def add_in_psum(i, t0, t1, banks):
+            there = bank(banks[0], "there%d_%d" % (i, t0))
+            back = bank(banks[1], "back%d_%d" % (i, t0))
             for r in range(2):
-                for h, (t0, t1) in enumerate(halves):
-                    for t in range(t0, t1, P):
-                        nc.tensor.matmul(
-                            there[h][:, t - t0 : t - t0 + P],
-                            terms[i][r][:, t : t + P],
-                            ident[:],
-                            start=(r == 0 and t == t0),
-                            stop=(r == 1 and t == t1 - P),
-                            is_transpose=True,
-                        )
-            for h, (t0, t1) in enumerate(halves):
-                nc.scalar.copy(out=turned[i][:, t0:t1], in_=there[h][:, 0 : t1 - t0])
-            for h, (t0, t1) in enumerate(halves):
                 for t in range(t0, t1, P):
-                    nc.tensor.transpose(back[h][:, t - t0 : t - t0 + P], turned[i][:, t : t + P], ident[:])
-            for h, (t0, t1) in enumerate(halves):
-                nc.scalar.copy(out=o_sb[i][:, t0:t1], in_=back[h][:, 0 : t1 - t0])
-            store(i, 0, T)
+                    nc.tensor.matmul(
+                        there[:, t - t0 : t - t0 + P],
+                        terms[i][r][:, t : t + P],
+                        ident[:],
+                        start=(r == 0 and t == t0),
+                        stop=(r == 1 and t == t1 - P),
+                        is_transpose=True,
+                    )
+            nc.scalar.copy(out=turned[i][:, t0:t1], in_=there[:, 0 : t1 - t0])
+            for t in range(t0, t1, P):
+                nc.tensor.transpose(back[:, t - t0 : t - t0 + P], turned[i][:, t : t + P], ident[:])
+            nc.scalar.copy(out=o_sb[i][:, t0:t1], in_=back[:, 0 : t1 - t0])
+            store(i, t0, t1)
 
         fetch(0, 0, 0, T)
         fetch(0, 1, 0, T)
-        add_in_psum(0, (6, 7, 4, 0))
+        add_in_psum(0, 0, 384, (4, 5))
+        add_in_psum(0, 384, T, (6, 7))
         fetch(1, 0, 0, T)
-        fetch(1, 1, 0, T)
-        add_in_psum(1, (1, 2, 3, 5))
+        fetch(1, 1, 0, 384)
+        add_in_psum(1, 0, 384, (1, 3))
+        fetch(1, 1, 384, T)
+        add_in_psum(1, 384, T, (0, 2))
         fetch(2, 0, 0, T)
         fetch(2, 1, 0, 384)
         fetch(2, 1, 384, T)

@@ -18,9 +18,8 @@ MULT = mybir.AluOpType.mult
 ADD = mybir.AluOpType.add
 
 P = 128
-TOKEN_LOADS = ((0, 256), (256, 256), (512, 128))
 TOKEN_GROUPS = ((0, 256), (256, 128), (384, 128), (512, 128))
-SLOT_CHUNKS = ((0, 448), (448, 448), (896, 384))
+FIRST_CHUNKS = ((0, 448), (448, 448), (896, 384))
 SLOT_GROUPS = ((0, 256), (256, 256), (512, 256), (768, 256), (1024, 128), (1152, 128))
 
 
@@ -34,16 +33,21 @@ def tile_moe_prv_lin_none_kernel(tc, uT, wu, w_words, w_scales, gate, offs, pos1
             return psum.tile([P, 512], F32, name=name, tag="bank%d" % b)
 
         wu_rows = wu.rearrange("(p j) c -> p j c", j=4)
-        u_rows = uT.rearrange("(p j) t -> p j t", j=4)
         wu_raw = [keep.tile([P, 4, 256], F32, name="wu_raw%d" % h) for h in range(2)]
         for h in range(2):
             nc.sync.dma_start(out=wu_raw[h][:], in_=wu_rows[:, :, 256 * h : 256 * (h + 1)])
-        u_raw = [keep.tile([P, 4, w], F32, name="u_raw%d" % c) for c, (t0, w) in enumerate(TOKEN_LOADS)]
-        for c, (t0, w) in enumerate(TOKEN_LOADS):
+        u_rows = uT.rearrange("(p j) t -> p j t", j=4)
+        u_raw = [keep.tile([P, 4, w], F32, name="u_raw%d" % c, tag="u_raw%d" % c) for c, (t0, w) in enumerate(TOKEN_GROUPS)]
+        for c, (t0, w) in enumerate(TOKEN_GROUPS):
             nc.sync.dma_start(out=u_raw[c][:], in_=u_rows[:, :, t0 : t0 + w])
         offs_sb = keep.tile([P, S // 16], U16, name="offs_sb")
         nc.sync.dma_start(offs_sb[:], offs)
 
+        w_codes = keep.tile([P, E, N], U32, name="w_codes", align_bytes=64)
+        nc.sync.dma_start(
+            out=w_codes[:].bitcast(I32),
+            in_=w_words[:, 0, :, :, :].rearrange("e p n r -> p e (n r)").bitcast(I32),
+        )
         w_plane = keep.tile([P, E, N], U8, name="w_plane", align_bytes=64)
         nc.gpsimd.memset(w_plane[:].bitcast(I32), 0)
         ident = keep.tile([P, P], F32, name="ident")
@@ -53,36 +57,29 @@ def tile_moe_prv_lin_none_kernel(tc, uT, wu, w_words, w_scales, gate, offs, pos1
                 out=w_plane[32 * q : 32 * q + 4, :, :].bitcast(I32),
                 in_=w_scales[:, 0, 4 * q : 4 * q + 4, :].rearrange("e q n -> q e n").bitcast(I32),
             )
-        w_codes = keep.tile([P, E, N], U32, name="w_codes", align_bytes=64)
-        nc.sync.dma_start(
-            out=w_codes[:].bitcast(I32),
-            in_=w_words[:, 0, :, :, :].rearrange("e p n r -> p e (n r)").bitcast(I32),
-        )
         pos1_sb = keep.tile([P, T // 16], U16, name="pos1_sb")
         nc.sync.dma_start(pos1_sb[:], pos1)
         pos2_sb = keep.tile([P, T // 16], U16, name="pos2_sb")
         nc.sync.dma_start(pos2_sb[:], pos2)
-        gate_sb = [keep.tile([P, 2, T], F32, name="gate%d" % i) for i in range(3)]
-        for i in range(3):
-            nc.sync.dma_start(out=gate_sb[i][:], in_=gate[:, P * i : P * (i + 1), :].rearrange("r p t -> p r t"))
+        gate_sb = keep.tile([P, 2, T], F32, name="gate_sb")
+        nc.sync.dma_start(out=gate_sb[:], in_=gate[:, 0:P, :].rearrange("r p t -> p r t"))
 
-        x_pairs = [keep.tile([P, T, 2], BF16, name="x_pairs%d" % u) for u in range(2)]
+        x_pairs = [keep.tile([P, T, 2], BF16, name="x_pairs%d" % u, tag=("u_raw3", "x_pairs1")[u]) for u in range(2)]
+        wu_bf = [keep.tile([P, 2, P, 4], BF16, name="wu_bf%d" % u, align_bytes=64) for u in range(2)]
+        wu_codes = [keep.tile([P, 2, P], U32, name="wu_codes%d" % u, align_bytes=64) for u in range(2)]
+        wu_plane = [keep.tile([P, 2, P], U8, name="wu_plane%d" % u, align_bytes=64) for u in range(2)]
 
-        wu_bf = keep.tile([P, 4, P, 4], BF16, name="wu_bf", align_bytes=64)
-        wu_codes = keep.tile([P, 4, P], U32, name="wu_codes", align_bytes=64)
-        wu_plane = keep.tile([P, 4, P], U8, name="wu_plane", align_bytes=64)
-
-        def wu_views(h, a, b):
+        def wu_views(u, h):
             return dict(
-                out=wu_bf[:].rearrange("p t m j -> p m j t")[:, 64 * h + a : 64 * h + b, :, :],
-                in_=wu_raw[h][:].rearrange("p j (m t) -> p m j t", t=4)[:, a:b, :, :],
+                out=wu_bf[u][:].rearrange("p e m j -> p m j e")[:, 64 * h : 64 * (h + 1), :, :],
+                in_=wu_raw[h][:].rearrange("p j (m t) -> p m j t", t=4)[:, :, :, 2 * u : 2 * u + 2],
             )
 
         def wu_quantize(u):
             nc.vector.quantize_mx(
-                out=wu_codes[:, 2 * u : 2 * u + 2, :].rearrange("p t m -> p (t m)").bitcast(FP8X4),
-                scales=wu_plane[:, 2 * u : 2 * u + 2, :].rearrange("p t m -> p (t m)"),
-                in_=wu_bf[:, 2 * u : 2 * u + 2, :, :].rearrange("p t m j -> p (t m j)"),
+                out=wu_codes[u][:].rearrange("p e m -> p (e m)").bitcast(FP8X4),
+                scales=wu_plane[u][:].rearrange("p e m -> p (e m)"),
+                in_=wu_bf[u][:].rearrange("p e m j -> p (e m j)"),
             )
 
         u_bf = [keep.tile([P, w, 4], BF16, name="u_bf%d" % c, align_bytes=64) for c, (t0, w) in enumerate(TOKEN_GROUPS)]
@@ -90,10 +87,9 @@ def tile_moe_prv_lin_none_kernel(tc, uT, wu, w_words, w_scales, gate, offs, pos1
         u_plane = keep.tile([P, T], U8, name="u_plane", align_bytes=64)
 
         def u_views(c, a, b):
-            load, lo = divmod(TOKEN_GROUPS[c][0], 256)
             return dict(
                 out=u_bf[c][:, a:b, :].rearrange("p (g i) j -> p g j i", i=4),
-                in_=u_raw[load][:, :, lo + a : lo + b].rearrange("p j (g i) -> p g j i", i=4),
+                in_=u_raw[c][:, :, a:b].rearrange("p j (g i) -> p g j i", i=4),
             )
 
         def u_quantize(c):
@@ -106,11 +102,10 @@ def tile_moe_prv_lin_none_kernel(tc, uT, wu, w_words, w_scales, gate, offs, pos1
 
         def project(u, t0, w, sums):
             for e in range(2):
-                t = 2 * u + e
                 nc.tensor.matmul_mx(
                     out=sums[:, e * w : (e + 1) * w],
-                    lhsT=wu_codes[:, t, :].bitcast(FP8X4),
-                    lhsT_scale=wu_plane[:, t, :],
+                    lhsT=wu_codes[u][:, e, :].bitcast(FP8X4),
+                    lhsT_scale=wu_plane[u][:, e, :],
                     rhs=u_codes[:, t0 : t0 + w].bitcast(FP8X4),
                     rhs_scale=u_plane[:, t0 : t0 + w],
                     start=True,
@@ -119,41 +114,40 @@ def tile_moe_prv_lin_none_kernel(tc, uT, wu, w_words, w_scales, gate, offs, pos1
             return dict(out=x_pairs[u][:, t0 : t0 + w, :], in_=sums.rearrange("p (e t) -> p t e", e=2))
 
         for h in range(2):
-            nc.vector.tensor_copy(**wu_views(h, 0, 40))
-            nc.scalar.copy(**wu_views(h, 40, 64))
+            nc.vector.tensor_copy(**wu_views(0, h))
+            nc.scalar.copy(**wu_views(1, h))
         wu_quantize(0)
-        nc.vector.tensor_copy(**u_views(0, 0, 144))
-        nc.scalar.copy(**u_views(0, 144, 256))
         wu_quantize(1)
+        nc.vector.tensor_copy(**u_views(0, 0, 160))
+        nc.scalar.copy(**u_views(0, 160, 256))
         u_quantize(0)
-        x_banks = [bank(b, "x_bank%d" % b) for b in range(6)]
-        nc.scalar.copy(**project(0, 0, 256, x_banks[0][:]))
-        nc.vector.tensor_copy(**u_views(1, 0, 128))
-        nc.scalar.copy(**u_views(2, 0, 128))
-        nc.vector.tensor_copy(**u_views(3, 0, 128))
-        for c in (1, 2, 3):
-            u_quantize(c)
-        nc.vector.tensor_copy(**project(0, 256, 128, x_banks[1][:, 0:256]))
-        nc.vector.tensor_copy(**project(0, 384, 128, x_banks[2][:, 0:256]))
-        nc.scalar.copy(**project(0, 512, 128, x_banks[3][:, 0:256]))
-        nc.scalar.copy(**project(1, 0, 256, x_banks[4][:]))
-        nc.scalar.copy(**project(1, 384, 256, x_banks[5][:]))
-        nc.scalar.copy(**project(1, 256, 128, x_banks[3][:, 256:512]))
+        nc.scalar.copy(**u_views(1, 0, 128))
+        nc.vector.tensor_copy(**u_views(2, 0, 128))
+        u_quantize(1)
+        nc.vector.tensor_copy(**u_views(3, 0, 80))
+        nc.scalar.copy(**u_views(3, 80, 128))
+        u_quantize(2)
+        u_quantize(3)
+        nc.scalar.copy(**project(0, 0, 256, bank(0, "x0_a")[:]))
+        nc.vector.tensor_copy(**project(0, 256, 128, bank(1, "x0_b")[:, 0:256]))
+        nc.vector.tensor_copy(**project(0, 384, 128, bank(2, "x0_c")[:, 0:256]))
+        nc.scalar.copy(**project(0, 512, 128, bank(3, "x0_d")[:, 0:256]))
+        nc.scalar.copy(**project(1, 0, 256, bank(2, "x1_a")[:]))
+        nc.scalar.copy(**project(1, 256, 256, bank(3, "x1_b")[:]))
+        nc.scalar.copy(**project(1, 512, 128, bank(2, "x1_c")[:, 0:256]))
 
-        xs_planes = [keep.tile([P, 2, n], U32, name="xs_planes%d" % c) for c, (s0, n) in enumerate(SLOT_CHUNKS)]
+        xs_planes = keep.tile([P, 2, S], U32, name="xs_planes")
         xs_bf = keep.tile([P, S, 4], BF16, name="xs_bf", align_bytes=64)
         xs_codes = keep.tile([P, S], U32, name="xs_codes", align_bytes=64)
         xs_plane = keep.tile([P, S], U8, name="xs_plane", align_bytes=64)
 
-        def gather_x(c, u):
-            s0, n = SLOT_CHUNKS[c]
+        def gather_x(u, s0, n):
             window = x_pairs[u][:].rearrange("p t e -> p (t e)").bitcast(U32)
-            nc.vector.tensor_copy(xs_planes[c][:, u, :], window.indirect(offs_sb[:, s0 // 16 : (s0 + n) // 16]))
+            nc.vector.tensor_copy(xs_planes[:, u, s0 : s0 + n], window.indirect(offs_sb[:, s0 // 16 : (s0 + n) // 16]))
 
-        def interleave(c):
-            s0, n = SLOT_CHUNKS[c]
-            words = xs_bf[:].rearrange("p s j -> p (s j)").bitcast(F32).rearrange("p (s u) -> p s u", u=2)
-            nc.scalar.copy(out=words[:, s0 : s0 + n, :], in_=xs_planes[c][:].bitcast(F32).rearrange("p u s -> p s u"))
+        def interleave(s0, n):
+            words = xs_bf[:].rearrange("p s j -> p (s j)").bitcast(U32).rearrange("p (s u) -> p s u", u=2)
+            nc.scalar.copy(out=words[:, s0 : s0 + n, :], in_=xs_planes[:, :, s0 : s0 + n].rearrange("p u s -> p s u"))
 
         def xs_quantize(s0, n):
             nc.vector.quantize_mx(
@@ -164,46 +158,38 @@ def tile_moe_prv_lin_none_kernel(tc, uT, wu, w_words, w_scales, gate, offs, pos1
 
         y_sb = [keep.tile([P, S], F32, name="y_sb%d" % i) for i in range(3)]
 
-        def expert(i, s0, n, sums):
-            e = s0 // C
-            nc.tensor.matmul_mx(
-                out=sums,
-                lhsT=w_codes[:, e, P * i : P * (i + 1)].bitcast(FP8X4),
-                lhsT_scale=w_plane[:, e, P * i : P * (i + 1)],
-                rhs=xs_codes[:, s0 : s0 + n].bitcast(FP8X4),
-                rhs_scale=xs_plane[:, s0 : s0 + n],
-                start=True,
-                stop=True,
-            )
-
         def experts(i, s0, n, step, sums):
             for a in range(0, n, step):
-                expert(i, s0 + a, step, sums[:, a : a + step])
+                e = (s0 + a) // C
+                nc.tensor.matmul_mx(
+                    out=sums[:, a : a + step],
+                    lhsT=w_codes[:, e, P * i : P * (i + 1)].bitcast(FP8X4),
+                    lhsT_scale=w_plane[:, e, P * i : P * (i + 1)],
+                    rhs=xs_codes[:, s0 + a : s0 + a + step].bitcast(FP8X4),
+                    rhs_scale=xs_plane[:, s0 + a : s0 + a + step],
+                    start=True,
+                    stop=True,
+                )
             return dict(out=y_sb[i][:, s0 : s0 + n], in_=sums)
 
-        gather_x(0, 0)
-        gather_x(1, 0)
-        gather_x(0, 1)
-        interleave(0)
-        gather_x(1, 1)
-        interleave(1)
-        gather_x(2, 0)
-        gather_x(2, 1)
-        interleave(2)
+        for s0, n in FIRST_CHUNKS:
+            gather_x(0, s0, n)
+        for e in range(E):
+            gather_x(1, e * C, C)
+            interleave(e * C, C)
         for s0, n in SLOT_GROUPS:
             xs_quantize(s0, n)
-        y0 = [bank(b, "y0_bank%d" % b) for b in range(5)]
-        nc.scalar.copy(**experts(0, 0, 512, C, y0[0][:]))
-        nc.scalar.copy(**experts(0, 512, C, C, y0[1][:, 0:C]))
-        nc.vector.tensor_copy(**experts(0, 768, C, C, y0[2][:, 0:C]))
-        nc.vector.tensor_copy(**experts(0, 1024, P, P, y0[4][:, 0:P]))
-        nc.vector.tensor_copy(**experts(0, 1152, P, P, y0[3][:, 0:P]))
-        nc.scalar.copy(**experts(1, 0, 512, C, bank(0, "y1_a")[:]))
-        nc.scalar.copy(**experts(1, 512, 512, C, bank(2, "y1_b")[:]))
-        nc.scalar.copy(**experts(1, 1024, C, C, y0[3][:, C:512]))
-        nc.scalar.copy(**experts(2, 1024, C, C, y0[1][:, C:512]))
-        nc.scalar.copy(**experts(2, 0, 512, C, bank(0, "y2_a")[:]))
-        nc.scalar.copy(**experts(2, 512, 512, C, bank(2, "y2_b")[:]))
+        for e in range(3):
+            nc.scalar.copy(**experts(0, e * C, C, C, bank(e, "y0_%d" % e)[:, 0:C]))
+        nc.vector.tensor_copy(**experts(0, 768, C, C, bank(3, "y0_3")[:, 0:C]))
+        nc.scalar.copy(**experts(0, 1024, P, P, bank(4, "y0_4")[:, 0:P]))
+        nc.scalar.copy(**experts(0, 1152, P, P, bank(5, "y0_5")[:, 0:P]))
+        nc.scalar.copy(**experts(1, 0, 512, C, bank(4, "y1_a")[:]))
+        nc.scalar.copy(**experts(1, 512, 512, C, bank(5, "y1_b")[:]))
+        nc.scalar.copy(**experts(1, 1024, C, C, bank(3, "y1_c")[:, 0:C]))
+        nc.scalar.copy(**experts(2, 0, 512, C, bank(3, "y2_a")[:]))
+        nc.scalar.copy(**experts(2, 512, 512, C, bank(4, "y2_b")[:]))
+        nc.scalar.copy(**experts(2, 1024, C, C, bank(5, "y2_c")[:, 0:C]))
 
         terms = [[keep.tile([P, T], F32, name="term%d%d" % (i, r)) for r in range(2)] for i in range(3)]
         o_sb = [keep.tile([P, T], F32, name="o_sb%d" % i) for i in range(3)]
@@ -212,7 +198,7 @@ def tile_moe_prv_lin_none_kernel(tc, uT, wu, w_words, w_scales, gate, offs, pos1
 
         def fetch(i, r, t0, t1):
             nc.vector.tensor_tensor(
-                terms[i][r][:, t0:t1], y_sb[i][:].indirect(lists[r][:, t0 // 16 : t1 // 16]), gate_sb[i][:, r, t0:t1], MULT
+                terms[i][r][:, t0:t1], y_sb[i][:].indirect(lists[r][:, t0 // 16 : t1 // 16]), gate_sb[:, r, t0:t1], MULT
             )
 
         def store(i, t0, t1):
@@ -243,15 +229,17 @@ def tile_moe_prv_lin_none_kernel(tc, uT, wu, w_words, w_scales, gate, offs, pos1
 
         fetch(0, 0, 0, T)
         fetch(0, 1, 0, T)
-        add_in_psum(0, 0, 384, (4, 5))
+        add_in_psum(0, 0, 384, (0, 1))
         add_in_psum(0, 384, T, (6, 7))
         fetch(1, 0, 0, T)
         fetch(1, 1, 0, 384)
-        add_in_psum(1, 0, 384, (1, 3))
+        add_in_psum(1, 0, 384, (2, 3))
         fetch(1, 1, 384, T)
-        add_in_psum(1, 384, T, (0, 2))
+        add_in_psum(1, 384, T, (4, 5))
         fetch(2, 0, 0, T)
-        fetch(2, 1, 0, 384)
-        fetch(2, 1, 384, T)
-        add_on_vector(2, 0, 384)
-        add_on_vector(2, 384, T)
+        fetch(2, 1, 0, 256)
+        fetch(2, 1, 256, 512)
+        add_on_vector(2, 0, 256)
+        fetch(2, 1, 512, T)
+        add_on_vector(2, 256, 512)
+        add_on_vector(2, 512, T)

@@ -16,10 +16,11 @@ U8 = mybir.dt.uint8
 FP8X4 = mybir.dt.float8_e4m3fn_x4
 MULT = mybir.AluOpType.mult
 ADD = mybir.AluOpType.add
+COPY = mybir.ActivationFunctionType.Copy
 
 P = 128
 TOKEN_GROUPS = ((0, 256), (256, 128), (384, 128), (512, 128))
-FIRST_CHUNKS = ((0, 448), (448, 448), (896, 384))
+SPLIT = 768
 SLOT_GROUPS = ((0, 256), (256, 256), (512, 256), (768, 256), (1024, 128), (1152, 128))
 
 
@@ -37,7 +38,7 @@ def tile_moe_prv_lin_none_kernel(tc, uT, wu, w_words, w_scales, gate, offs, pos1
         for h in range(2):
             nc.sync.dma_start(out=wu_raw[h][:], in_=wu_rows[:, :, 256 * h : 256 * (h + 1)])
         u_rows = uT.rearrange("(p j) t -> p j t", j=4)
-        u_raw = [keep.tile([P, 4, w], F32, name="u_raw%d" % c, tag="u_raw%d" % c) for c, (t0, w) in enumerate(TOKEN_GROUPS)]
+        u_raw = [keep.tile([P, 4, w], F32, name="u_raw%d" % c, tag="u_raw%d" % c, align_bytes=32) for c, (t0, w) in enumerate(TOKEN_GROUPS)]
         for c, (t0, w) in enumerate(TOKEN_GROUPS):
             nc.sync.dma_start(out=u_raw[c][:], in_=u_rows[:, :, t0 : t0 + w])
         offs_sb = keep.tile([P, S // 16], U16, name="offs_sb")
@@ -64,7 +65,7 @@ def tile_moe_prv_lin_none_kernel(tc, uT, wu, w_words, w_scales, gate, offs, pos1
         gate_sb = keep.tile([P, 2, T], F32, name="gate_sb")
         nc.sync.dma_start(out=gate_sb[:], in_=gate[:, 0:P, :].rearrange("r p t -> p r t"))
 
-        x_pairs = [keep.tile([P, T, 2], BF16, name="x_pairs%d" % u, tag=("u_raw3", "x_pairs1")[u]) for u in range(2)]
+        x_pairs = [keep.tile([P, T, 2], BF16, name="x_pairs%d" % u, tag=("u_raw3", "x_pairs1")[u], align_bytes=(32, 64)[u]) for u in range(2)]
         wu_bf = [keep.tile([P, 2, P, 4], BF16, name="wu_bf%d" % u, align_bytes=64) for u in range(2)]
         wu_codes = [keep.tile([P, 2, P], U32, name="wu_codes%d" % u, align_bytes=64) for u in range(2)]
         wu_plane = [keep.tile([P, 2, P], U8, name="wu_plane%d" % u, align_bytes=64) for u in range(2)]
@@ -132,22 +133,33 @@ def tile_moe_prv_lin_none_kernel(tc, uT, wu, w_words, w_scales, gate, offs, pos1
         nc.vector.tensor_copy(**project(0, 256, 128, bank(1, "x0_b")[:, 0:256]))
         nc.vector.tensor_copy(**project(0, 384, 128, bank(2, "x0_c")[:, 0:256]))
         nc.scalar.copy(**project(0, 512, 128, bank(3, "x0_d")[:, 0:256]))
+        nc.scalar.copy(**project(1, 512, 128, bank(1, "x1_c")[:, 0:256]))
         nc.scalar.copy(**project(1, 0, 256, bank(2, "x1_a")[:]))
         nc.scalar.copy(**project(1, 256, 256, bank(3, "x1_b")[:]))
-        nc.scalar.copy(**project(1, 512, 128, bank(2, "x1_c")[:, 0:256]))
+        x_single = keep.tile([P, 2, T], BF16, name="x_single")
+        for t0, t1, engine in ((0, 384, nc.vector), (384, T, nc.gpsimd)):
+            engine.tensor_copy(out=x_single[:, :, t0:t1], in_=x_pairs[0][:, t0:t1, :].rearrange("p t e -> p e t"))
 
-        xs_planes = keep.tile([P, 2, S], U32, name="xs_planes")
+        xs_head = keep.tile([P, 2, SPLIT], U32, name="xs_head")
+        xs_tail = [keep.tile([P, 2, C], U32, name="xs_tail%d" % ex) for ex in range(2)]
         xs_bf = keep.tile([P, S, 4], BF16, name="xs_bf", align_bytes=64)
-        xs_codes = keep.tile([P, S], U32, name="xs_codes", align_bytes=64)
+        xs_codes = keep.tile([P, S], U32, name="xs_codes", tag="x_pairs1", align_bytes=64)
         xs_plane = keep.tile([P, S], U8, name="xs_plane", align_bytes=64)
+
+        def planes(s0, n):
+            return xs_head[:, :, s0 : s0 + n] if s0 < SPLIT else xs_tail[(s0 - SPLIT) // C][:]
 
         def gather_x(u, s0, n):
             window = x_pairs[u][:].rearrange("p t e -> p (t e)").bitcast(U32)
-            nc.vector.tensor_copy(xs_planes[:, u, s0 : s0 + n], window.indirect(offs_sb[:, s0 // 16 : (s0 + n) // 16]))
+            nc.vector.tensor_copy(planes(s0, n)[:, u, :], window.indirect(offs_sb[:, s0 // 16 : (s0 + n) // 16]))
+
+        def gather_single(e, s0, n):
+            halves = planes(s0, n)[:, 0, :].bitcast(BF16).rearrange("p (s e) -> p s e", e=2)
+            nc.scalar.activation(halves[:, :, e], x_single[:, e, :].indirect(offs_sb[:, s0 // 16 : (s0 + n) // 16]), COPY)
 
         def interleave(s0, n):
             words = xs_bf[:].rearrange("p s j -> p (s j)").bitcast(U32).rearrange("p (s u) -> p s u", u=2)
-            nc.scalar.copy(out=words[:, s0 : s0 + n, :], in_=xs_planes[:, :, s0 : s0 + n].rearrange("p u s -> p s u"))
+            return dict(out=words[:, s0 : s0 + n, :], in_=planes(s0, n).rearrange("p u s -> p s u"))
 
         def xs_quantize(s0, n):
             nc.vector.quantize_mx(
@@ -172,16 +184,23 @@ def tile_moe_prv_lin_none_kernel(tc, uT, wu, w_words, w_scales, gate, offs, pos1
                 )
             return dict(out=y_sb[i][:, s0 : s0 + n], in_=sums)
 
-        for s0, n in FIRST_CHUNKS:
-            gather_x(0, s0, n)
-        for e in range(E):
-            gather_x(1, e * C, C)
-            interleave(e * C, C)
+        gather_x(0, 0, 384)
+        gather_x(0, 384, 384)
+        for ex in (3, 4):
+            for e in range(2):
+                gather_single(e, ex * C, C)
+        for ex in range(E):
+            gather_x(1, ex * C, C)
+            if ex < 3:
+                nc.gpsimd.tensor_copy(**interleave(ex * C, C))
+            else:
+                nc.scalar.copy(**interleave(ex * C, C))
         for s0, n in SLOT_GROUPS:
             xs_quantize(s0, n)
-        for e in range(3):
+        for e in range(2):
             nc.scalar.copy(**experts(0, e * C, C, C, bank(e, "y0_%d" % e)[:, 0:C]))
-        nc.vector.tensor_copy(**experts(0, 768, C, C, bank(3, "y0_3")[:, 0:C]))
+        for e in range(2, 4):
+            nc.vector.tensor_copy(**experts(0, e * C, C, C, bank(e, "y0_%d" % e)[:, 0:C]))
         nc.scalar.copy(**experts(0, 1024, P, P, bank(4, "y0_4")[:, 0:P]))
         nc.scalar.copy(**experts(0, 1152, P, P, bank(5, "y0_5")[:, 0:P]))
         nc.scalar.copy(**experts(1, 0, 512, C, bank(4, "y1_a")[:]))
@@ -227,15 +246,11 @@ def tile_moe_prv_lin_none_kernel(tc, uT, wu, w_words, w_scales, gate, offs, pos1
             nc.scalar.copy(out=o_sb[i][:, t0:t1], in_=back[:, 0 : t1 - t0])
             store(i, t0, t1)
 
-        fetch(0, 0, 0, T)
-        fetch(0, 1, 0, T)
-        add_in_psum(0, 0, 384, (0, 1))
-        add_in_psum(0, 384, T, (6, 7))
-        fetch(1, 0, 0, T)
-        fetch(1, 1, 0, 384)
-        add_in_psum(1, 0, 384, (2, 3))
-        fetch(1, 1, 384, T)
-        add_in_psum(1, 384, T, (4, 5))
+        for i, banks in enumerate((((0, 1), (6, 7)), ((2, 3), (4, 5)))):
+            for (t0, t1), pair in zip(((0, 384), (384, T)), banks):
+                fetch(i, 0, t0, t1)
+                fetch(i, 1, t0, t1)
+                add_in_psum(i, t0, t1, pair)
         fetch(2, 0, 0, T)
         fetch(2, 1, 0, 256)
         fetch(2, 1, 256, 512)

@@ -19,6 +19,7 @@ ADD = mybir.AluOpType.add
 COPY = mybir.ActivationFunctionType.Copy
 
 P = 128
+TOKEN_LOADS = ((0, 256), (256, 256), (512, 128))
 TOKEN_GROUPS = ((0, 256), (256, 128), (384, 128), (512, 128))
 SPLIT = 768
 SLOT_GROUPS = ((0, 256), (256, 256), (512, 256), (768, 256), (1024, 128), (1152, 128))
@@ -34,12 +35,12 @@ def tile_moe_prv_lin_none_kernel(tc, uT, wu, w_words, w_scales, gate, offs, pos1
             return psum.tile([P, 512], F32, name=name, tag="bank%d" % b)
 
         wu_rows = wu.rearrange("(p j) c -> p j c", j=4)
-        wu_raw = [keep.tile([P, 4, 256], F32, name="wu_raw%d" % h) for h in range(2)]
+        wu_raw = [keep.tile([P, 2, K], F32, name="wu_raw%d" % h) for h in range(2)]
         for h in range(2):
-            nc.sync.dma_start(out=wu_raw[h][:], in_=wu_rows[:, :, 256 * h : 256 * (h + 1)])
+            nc.sync.dma_start(out=wu_raw[h][:], in_=wu_rows[:, 2 * h : 2 * h + 2, :])
         u_rows = uT.rearrange("(p j) t -> p j t", j=4)
-        u_raw = [keep.tile([P, 4, w], F32, name="u_raw%d" % c, tag="u_raw%d" % c, align_bytes=32) for c, (t0, w) in enumerate(TOKEN_GROUPS)]
-        for c, (t0, w) in enumerate(TOKEN_GROUPS):
+        u_raw = [keep.tile([P, 4, w], F32, name="u_raw%d" % c, tag="u_raw%d" % c, align_bytes=32) for c, (t0, w) in enumerate(TOKEN_LOADS)]
+        for c, (t0, w) in enumerate(TOKEN_LOADS):
             nc.sync.dma_start(out=u_raw[c][:], in_=u_rows[:, :, t0 : t0 + w])
         offs_sb = keep.tile([P, S // 16], U16, name="offs_sb")
         nc.sync.dma_start(offs_sb[:], offs)
@@ -65,14 +66,14 @@ def tile_moe_prv_lin_none_kernel(tc, uT, wu, w_words, w_scales, gate, offs, pos1
         gate_sb = keep.tile([P, 2, T], F32, name="gate_sb")
         nc.sync.dma_start(out=gate_sb[:], in_=gate[:, 0:P, :].rearrange("r p t -> p r t"))
 
-        x_pairs = [keep.tile([P, T, 2], BF16, name="x_pairs%d" % u, tag=("u_raw3", "x_pairs1")[u], align_bytes=(32, 64)[u]) for u in range(2)]
+        x_pairs = [keep.tile([P, T, 2], BF16, name="x_pairs%d" % u, tag=("u_raw2", "x_pairs1")[u], align_bytes=(32, 64)[u]) for u in range(2)]
         wu_bf = [keep.tile([P, 2, P, 4], BF16, name="wu_bf%d" % u, align_bytes=64) for u in range(2)]
         wu_codes = [keep.tile([P, 2, P], U32, name="wu_codes%d" % u, align_bytes=64) for u in range(2)]
         wu_plane = [keep.tile([P, 2, P], U8, name="wu_plane%d" % u, align_bytes=64) for u in range(2)]
 
         def wu_views(u, h):
             return dict(
-                out=wu_bf[u][:].rearrange("p e m j -> p m j e")[:, 64 * h : 64 * (h + 1), :, :],
+                out=wu_bf[u][:].rearrange("p e m j -> p m j e")[:, :, 2 * h : 2 * h + 2, :],
                 in_=wu_raw[h][:].rearrange("p j (m t) -> p m j t", t=4)[:, :, :, 2 * u : 2 * u + 2],
             )
 
@@ -88,9 +89,10 @@ def tile_moe_prv_lin_none_kernel(tc, uT, wu, w_words, w_scales, gate, offs, pos1
         u_plane = keep.tile([P, T], U8, name="u_plane", align_bytes=64)
 
         def u_views(c, a, b):
+            load, lo = divmod(TOKEN_GROUPS[c][0], 256)
             return dict(
                 out=u_bf[c][:, a:b, :].rearrange("p (g i) j -> p g j i", i=4),
-                in_=u_raw[c][:, :, a:b].rearrange("p j (g i) -> p g j i", i=4),
+                in_=u_raw[load][:, :, lo + a : lo + b].rearrange("p j (g i) -> p g j i", i=4),
             )
 
         def u_quantize(c):
@@ -122,11 +124,11 @@ def tile_moe_prv_lin_none_kernel(tc, uT, wu, w_words, w_scales, gate, offs, pos1
         nc.vector.tensor_copy(**u_views(0, 0, 160))
         nc.scalar.copy(**u_views(0, 160, 256))
         u_quantize(0)
-        nc.scalar.copy(**u_views(1, 0, 128))
-        nc.vector.tensor_copy(**u_views(2, 0, 128))
+        nc.vector.tensor_copy(**u_views(1, 0, 128))
+        nc.scalar.copy(**u_views(2, 0, 128))
         u_quantize(1)
-        nc.vector.tensor_copy(**u_views(3, 0, 80))
-        nc.scalar.copy(**u_views(3, 80, 128))
+        nc.vector.tensor_copy(**u_views(3, 0, 96))
+        nc.scalar.copy(**u_views(3, 96, 128))
         u_quantize(2)
         u_quantize(3)
         nc.scalar.copy(**project(0, 0, 256, bank(0, "x0_a")[:]))

@@ -22,7 +22,7 @@ P = 128
 TOKEN_LOADS = ((0, 256), (256, 256), (512, 128))
 TOKEN_GROUPS = ((0, 256), (256, 128), (384, 128), (512, 128))
 SPLIT = 768
-SLOT_GROUPS = ((0, 256), (256, 256), (512, 256), (768, 256), (1024, 128), (1152, 128))
+SLOT_GROUPS = ((0, 512), (512, 256), (768, 256), (1024, 128), (1152, 128))
 
 
 def tile_moe_prv_lin_none_kernel(tc, uT, wu, w_words, w_scales, gate, offs, pos1, pos2, out):
@@ -199,8 +199,7 @@ def tile_moe_prv_lin_none_kernel(tc, uT, wu, w_words, w_scales, gate, offs, pos1
                 nc.scalar.copy(**interleave(ex * C, C))
         for s0, n in SLOT_GROUPS:
             xs_quantize(s0, n)
-        for e in range(2):
-            nc.scalar.copy(**experts(0, e * C, C, C, bank(e, "y0_%d" % e)[:, 0:C]))
+        nc.scalar.copy(**experts(0, 0, 512, C, bank(0, "y0_0")[:]))
         for e in range(2, 4):
             nc.vector.tensor_copy(**experts(0, e * C, C, C, bank(e, "y0_%d" % e)[:, 0:C]))
         nc.scalar.copy(**experts(0, 1024, P, P, bank(4, "y0_4")[:, 0:P]))
@@ -248,11 +247,14 @@ def tile_moe_prv_lin_none_kernel(tc, uT, wu, w_words, w_scales, gate, offs, pos1
             nc.scalar.copy(out=o_sb[i][:, t0:t1], in_=back[:, 0 : t1 - t0])
             store(i, t0, t1)
 
-        for i, banks in enumerate((((0, 1), (6, 7)), ((2, 3), (4, 5)))):
-            for (t0, t1), pair in zip(((0, 384), (384, T)), banks):
-                fetch(i, 0, t0, t1)
-                fetch(i, 1, t0, t1)
-                add_in_psum(i, t0, t1, pair)
+        fetch(0, 0, 0, T)
+        fetch(0, 1, 0, T)
+        add_in_psum(0, 0, 384, (0, 1))
+        add_in_psum(0, 384, T, (6, 7))
+        for (t0, t1), banks in zip(((0, 384), (384, T)), ((2, 3), (4, 5))):
+            fetch(1, 0, t0, t1)
+            fetch(1, 1, t0, t1)
+            add_in_psum(1, t0, t1, banks)
         fetch(2, 0, 0, T)
         fetch(2, 1, 0, 256)
         fetch(2, 1, 256, 512)

@@ -211,9 +211,10 @@ def tile_moe_prv_lin_none_kernel(tc, uT, wu, w_words, w_scales, gate, offs, pos1
         nc.scalar.copy(**experts(2, 512, 512, C, bank(4, "y2_b")[:]))
         nc.scalar.copy(**experts(2, 1024, C, C, bank(5, "y2_c")[:, 0:C]))
 
-        terms = [[keep.tile([P, T], F32, name="term%d%d" % (i, r)) for r in range(2)] for i in range(3)]
+        terms = [[keep.tile([P, T], F32, name="term%d%d" % (i, r), tag="term%d%d" % (i, r)) for r in range(2)] for i in range(2)]
+        terms.append([keep.tile([P, T], F32, name="term20")])
         o_sb = [keep.tile([P, T], F32, name="o_sb%d" % i) for i in range(3)]
-        turned = [keep.tile([P, T], F32, name="turned%d" % i) for i in range(2)]
+        turned = [keep.tile([P, T], F32, name="turned%d" % i, tag="turned%d" % i) for i in range(2)]
         lists = (pos1_sb, pos2_sb)
 
         def fetch(i, r, t0, t1):
@@ -222,11 +223,7 @@ def tile_moe_prv_lin_none_kernel(tc, uT, wu, w_words, w_scales, gate, offs, pos1
             )
 
         def store(i, t0, t1):
-            nc.sync.dma_start(out=out[P * i : P * (i + 1), t0:t1], in_=o_sb[i][:, t0:t1])
-
-        def add_on_vector(i, t0, t1):
-            nc.vector.tensor_tensor(o_sb[i][:, t0:t1], terms[i][0][:, t0:t1], terms[i][1][:, t0:t1], ADD)
-            store(i, t0, t1)
+            nc.scalar.dma_start(out=out[P * i : P * (i + 1), t0:t1], in_=o_sb[i][:, t0:t1])
 
         def add_in_psum(i, t0, t1, banks):
             there = bank(banks[0], "there%d_%d" % (i, t0))
@@ -251,14 +248,24 @@ def tile_moe_prv_lin_none_kernel(tc, uT, wu, w_words, w_scales, gate, offs, pos1
         fetch(0, 1, 0, T)
         add_in_psum(0, 0, 384, (0, 1))
         add_in_psum(0, 384, T, (6, 7))
-        for (t0, t1), banks in zip(((0, 384), (384, T)), ((2, 3), (4, 5))):
+        for (t0, t1), banks in zip(((0, 384), (384, T)), ((0, 2), (6, 4))):
             fetch(1, 0, t0, t1)
             fetch(1, 1, t0, t1)
             add_in_psum(1, t0, t1, banks)
         fetch(2, 0, 0, T)
-        fetch(2, 1, 0, 256)
-        fetch(2, 1, 256, 512)
-        add_on_vector(2, 0, 256)
-        fetch(2, 1, 512, T)
-        add_on_vector(2, 256, 512)
-        add_on_vector(2, 512, T)
+        def last_fetch(t0, t1, tag):
+            piece = keep.tile([P, t1 - t0], F32, name="piece%d" % t0, tag=tag)
+            nc.vector.tensor_tensor(piece[:], y_sb[2][:].indirect(pos2_sb[:, t0 // 16 : t1 // 16]), gate_sb[:, 1, t0:t1], MULT)
+            return piece
+
+        def last_add(t0, t1, piece, total):
+            nc.vector.tensor_tensor(total, terms[2][0][:, t0:t1], piece[:], ADD)
+            nc.sync.dma_start(out=out[2 * P : 3 * P, t0:t1], in_=total)
+
+        piece_a = last_fetch(0, 384, "piece_even")
+        piece_b = last_fetch(384, 512, "piece_odd")
+        last_add(0, 384, piece_a, o_sb[2][:, 0:384])
+        piece_c = last_fetch(512, T, "term11")
+        o_tail = keep.tile([P, 256], F32, name="o_tail", tag="turned1")
+        last_add(384, 512, piece_b, o_tail[:, 0:P])
+        last_add(512, T, piece_c, o_tail[:, P : 2 * P])

@@ -211,61 +211,57 @@ def tile_moe_prv_lin_none_kernel(tc, uT, wu, w_words, w_scales, gate, offs, pos1
         nc.scalar.copy(**experts(2, 512, 512, C, bank(4, "y2_b")[:]))
         nc.scalar.copy(**experts(2, 1024, C, C, bank(5, "y2_c")[:, 0:C]))
 
-        terms = [[keep.tile([P, T], F32, name="term%d%d" % (i, r), tag="term%d%d" % (i, r)) for r in range(2)] for i in range(2)]
-        terms.append([keep.tile([P, T], F32, name="term20")])
-        o_sb = [keep.tile([P, T], F32, name="o_sb%d" % i) for i in range(3)]
-        turned = [keep.tile([P, T], F32, name="turned%d" % i, tag="turned%d" % i) for i in range(2)]
+        o_sb = [keep.tile([P, T], F32, name="o_sb%d" % i) for i in range(2)]
         lists = (pos1_sb, pos2_sb)
 
-        def fetch(i, r, t0, t1):
-            nc.vector.tensor_tensor(
-                terms[i][r][:, t0:t1], y_sb[i][:].indirect(lists[r][:, t0 // 16 : t1 // 16]), gate_sb[:, r, t0:t1], MULT
-            )
+        def fetch(i, r, t0, t1, term):
+            nc.vector.tensor_tensor(term, y_sb[i][:].indirect(lists[r][:, t0 // 16 : t1 // 16]), gate_sb[:, r, t0:t1], MULT)
 
-        def store(i, t0, t1):
-            nc.scalar.dma_start(out=out[P * i : P * (i + 1), t0:t1], in_=o_sb[i][:, t0:t1])
+        def fetch_both(i, t0, t1):
+            terms = [keep.tile([P, t1 - t0], F32, name="term%d%d_%d" % (i, r, t0), tag="term%d%d_%d" % (i, r, t0)) for r in range(2)]
+            for r in range(2):
+                fetch(i, r, t0, t1, terms[r][:])
+            return terms
 
-        def add_in_psum(i, t0, t1, banks):
+        def add_in_psum(i, t0, t1, terms, banks):
             there = bank(banks[0], "there%d_%d" % (i, t0))
             back = bank(banks[1], "back%d_%d" % (i, t0))
+            turned = keep.tile([P, t1 - t0], F32, name="turned%d_%d" % (i, t0), tag="turned%d_%d" % (i, t0))
             for r in range(2):
                 for t in range(t0, t1, P):
                     nc.tensor.matmul(
                         there[:, t - t0 : t - t0 + P],
-                        terms[i][r][:, t : t + P],
+                        terms[r][:, t - t0 : t - t0 + P],
                         ident[:],
                         start=(r == 0 and t == t0),
                         stop=(r == 1 and t == t1 - P),
                         is_transpose=True,
                     )
-            nc.scalar.copy(out=turned[i][:, t0:t1], in_=there[:, 0 : t1 - t0])
+            nc.scalar.copy(out=turned[:], in_=there[:, 0 : t1 - t0])
             for t in range(t0, t1, P):
-                nc.tensor.transpose(back[:, t - t0 : t - t0 + P], turned[i][:, t : t + P], ident[:])
+                nc.tensor.transpose(back[:, t - t0 : t - t0 + P], turned[:, t - t0 : t - t0 + P], ident[:])
             nc.scalar.copy(out=o_sb[i][:, t0:t1], in_=back[:, 0 : t1 - t0])
-            store(i, t0, t1)
+            (nc.sync, nc.scalar)[i].dma_start(out=out[P * i : P * (i + 1), t0:t1], in_=o_sb[i][:, t0:t1])
 
-        fetch(0, 0, 0, T)
-        fetch(0, 1, 0, T)
-        add_in_psum(0, 0, 384, (0, 1))
-        add_in_psum(0, 384, T, (6, 7))
-        for (t0, t1), banks in zip(((0, 384), (384, T)), ((0, 2), (6, 4))):
-            fetch(1, 0, t0, t1)
-            fetch(1, 1, t0, t1)
-            add_in_psum(1, t0, t1, banks)
-        fetch(2, 0, 0, T)
-        def last_fetch(t0, t1, tag):
-            piece = keep.tile([P, t1 - t0], F32, name="piece%d" % t0, tag=tag)
-            nc.vector.tensor_tensor(piece[:], y_sb[2][:].indirect(pos2_sb[:, t0 // 16 : t1 // 16]), gate_sb[:, 1, t0:t1], MULT)
-            return piece
-
-        def last_add(t0, t1, piece, total):
-            nc.vector.tensor_tensor(total, terms[2][0][:, t0:t1], piece[:], ADD)
+        def add_on_vector(t0, t1, total, first, second):
+            nc.vector.tensor_tensor(total, first, second, ADD)
             nc.sync.dma_start(out=out[2 * P : 3 * P, t0:t1], in_=total)
 
-        piece_a = last_fetch(0, 384, "piece_even")
-        piece_b = last_fetch(384, 512, "piece_odd")
-        last_add(0, 384, piece_a, o_sb[2][:, 0:384])
-        piece_c = last_fetch(512, T, "term11")
-        o_tail = keep.tile([P, 256], F32, name="o_tail", tag="turned1")
-        last_add(384, 512, piece_b, o_tail[:, 0:P])
-        last_add(512, T, piece_c, o_tail[:, P : 2 * P])
+        whole = fetch_both(0, 0, T)
+        add_in_psum(0, 0, 384, [term[:, 0:384] for term in whole], (0, 1))
+        add_in_psum(0, 384, T, [term[:, 384:T] for term in whole], (6, 7))
+        add_in_psum(1, 0, 384, fetch_both(1, 0, 384), (0, 2))
+        add_in_psum(1, 384, T, fetch_both(1, 384, T), (6, 4))
+
+        first = keep.tile([P, T], F32, name="first")
+        second = keep.tile([P, 512], F32, name="second")
+        fetch(2, 0, 0, T, first[:])
+        fetch(2, 1, 0, 384, second[:, 0:384])
+        fetch(2, 1, 384, 512, second[:, 384:512])
+        o_head = keep.tile([P, 384], F32, name="o_head", tag="term11_0")
+        add_on_vector(0, 384, o_head[:], first[:, 0:384], second[:, 0:384])
+        second_end = keep.tile([P, P], F32, name="second_end", tag="term11_384")
+        fetch(2, 1, 512, T, second_end[:])
+        o_tail = keep.tile([P, 256], F32, name="o_tail", tag="turned1_384")
+        add_on_vector(384, 512, o_tail[:, 0:P], first[:, 384:512], second[:, 384:512])
+        add_on_vector(512, T, o_tail[:, P : 2 * P], first[:, 512:T], second_end[:])

@@ -145,7 +145,7 @@ def tile_moe_prv_lin_none_kernel(tc, uT, wu, w_words, w_scales, gate, offs, pos1
         xs_head = keep.tile([P, 2, SPLIT], U32, name="xs_head")
         xs_tail = [keep.tile([P, 2, C], U32, name="xs_tail%d" % ex) for ex in range(2)]
         xs_bf = keep.tile([P, S, 4], BF16, name="xs_bf", align_bytes=64)
-        xs_codes = keep.tile([P, S], U32, name="xs_codes", tag="x_pairs1", align_bytes=64)
+        xs_codes = keep.tile([P, S], U32, name="xs_codes", align_bytes=64)
         xs_plane = keep.tile([P, S], U8, name="xs_plane", align_bytes=64)
 
         def planes(s0, n):

@@ -19,10 +19,17 @@ ADD = mybir.AluOpType.add
 COPY = mybir.ActivationFunctionType.Copy
 
 P = 128
-TOKEN_LOADS = ((0, 256), (256, 256), (512, 128))
+BANK = 512
+LOAD_WIDTH = 256
+TOKEN_LOADS = ((0, LOAD_WIDTH), (256, LOAD_WIDTH), (512, 128))
 TOKEN_GROUPS = ((0, 256), (256, 128), (384, 128), (512, 128))
-SPLIT = 768
-SLOT_GROUPS = ((0, 512), (512, 256), (768, 256), (1024, 128), (1152, 128))
+FIRST_GROUP_ON_VECTOR, LAST_GROUP_ON_VECTOR = 160, 96
+SINGLES_ON_VECTOR = 384
+HEAD_EXPERTS = 3
+SPLIT = HEAD_EXPERTS * C
+ON_GPSIMD = 2 * C + P
+SLOT_GROUPS = ((0, 2 * C), (2 * C, C), (3 * C, C), (4 * C, P), (4 * C + P, P))
+CUT = 384
 
 
 def tile_moe_prv_lin_none_kernel(tc, uT, wu, w_words, w_scales, gate, offs, pos1, pos2, out):
@@ -32,7 +39,7 @@ def tile_moe_prv_lin_none_kernel(tc, uT, wu, w_words, w_scales, gate, offs, pos1
         psum = ctx.enter_context(tc.psum_pool(name="psum", bufs=1))
 
         def bank(b, name):
-            return psum.tile([P, 512], F32, name=name, tag="bank%d" % b)
+            return psum.tile([P, BANK], F32, name=name, tag="bank%d" % b)
 
         wu_rows = wu.rearrange("(p j) c -> p j c", j=4)
         wu_raw = [keep.tile([P, 2, K], F32, name="wu_raw%d" % h) for h in range(2)]
@@ -50,13 +57,13 @@ def tile_moe_prv_lin_none_kernel(tc, uT, wu, w_words, w_scales, gate, offs, pos1
             out=w_codes[:].bitcast(I32),
             in_=w_words[:, 0, :, :, :].rearrange("e p n r -> p e (n r)").bitcast(I32),
         )
-        w_plane = keep.tile([P, E, N], U8, name="w_plane", align_bytes=64)
-        nc.gpsimd.memset(w_plane[:].bitcast(I32), 0)
+        w_scale = keep.tile([P, E, N], U8, name="w_scale", align_bytes=64)
+        nc.gpsimd.memset(w_scale[:].bitcast(I32), 0)
         ident = keep.tile([P, P], F32, name="ident")
         make_identity(nc, ident[:])
         for q in range(4):
             nc.sync.dma_start(
-                out=w_plane[32 * q : 32 * q + 4, :, :].bitcast(I32),
+                out=w_scale[32 * q : 32 * q + 4, :, :].bitcast(I32),
                 in_=w_scales[:, 0, 4 * q : 4 * q + 4, :].rearrange("e q n -> q e n").bitcast(I32),
             )
         pos1_sb = keep.tile([P, T // 16], U16, name="pos1_sb")
@@ -69,7 +76,7 @@ def tile_moe_prv_lin_none_kernel(tc, uT, wu, w_words, w_scales, gate, offs, pos1
         x_pairs = [keep.tile([P, T, 2], BF16, name="x_pairs%d" % u, tag=("u_raw2", "x_pairs1")[u], align_bytes=(32, 64)[u]) for u in range(2)]
         wu_bf = [keep.tile([P, 2, P, 4], BF16, name="wu_bf%d" % u, align_bytes=64) for u in range(2)]
         wu_codes = [keep.tile([P, 2, P], U32, name="wu_codes%d" % u, align_bytes=64) for u in range(2)]
-        wu_plane = [keep.tile([P, 2, P], U8, name="wu_plane%d" % u, align_bytes=64) for u in range(2)]
+        wu_scale = [keep.tile([P, 2, P], U8, name="wu_scale%d" % u, align_bytes=64) for u in range(2)]
 
         def wu_views(u, h):
             return dict(
@@ -80,16 +87,16 @@ def tile_moe_prv_lin_none_kernel(tc, uT, wu, w_words, w_scales, gate, offs, pos1
         def wu_quantize(u):
             nc.vector.quantize_mx(
                 out=wu_codes[u][:].rearrange("p e m -> p (e m)").bitcast(FP8X4),
-                scales=wu_plane[u][:].rearrange("p e m -> p (e m)"),
+                scales=wu_scale[u][:].rearrange("p e m -> p (e m)"),
                 in_=wu_bf[u][:].rearrange("p e m j -> p (e m j)"),
             )
 
         u_bf = [keep.tile([P, w, 4], BF16, name="u_bf%d" % c, align_bytes=64) for c, (t0, w) in enumerate(TOKEN_GROUPS)]
         u_codes = keep.tile([P, T], U32, name="u_codes", align_bytes=64)
-        u_plane = keep.tile([P, T], U8, name="u_plane", align_bytes=64)
+        u_scale = keep.tile([P, T], U8, name="u_scale", align_bytes=64)
 
         def u_views(c, a, b):
-            load, lo = divmod(TOKEN_GROUPS[c][0], 256)
+            load, lo = divmod(TOKEN_GROUPS[c][0], LOAD_WIDTH)
             return dict(
                 out=u_bf[c][:, a:b, :].rearrange("p (g i) j -> p g j i", i=4),
                 in_=u_raw[load][:, :, lo + a : lo + b].rearrange("p j (g i) -> p g j i", i=4),
@@ -99,7 +106,7 @@ def tile_moe_prv_lin_none_kernel(tc, uT, wu, w_words, w_scales, gate, offs, pos1
             t0, w = TOKEN_GROUPS[c]
             nc.vector.quantize_mx(
                 out=u_codes[:, t0 : t0 + w].bitcast(FP8X4),
-                scales=u_plane[:, t0 : t0 + w],
+                scales=u_scale[:, t0 : t0 + w],
                 in_=u_bf[c][:].rearrange("p w j -> p (w j)"),
             )
 
@@ -108,9 +115,9 @@ def tile_moe_prv_lin_none_kernel(tc, uT, wu, w_words, w_scales, gate, offs, pos1
                 nc.tensor.matmul_mx(
                     out=sums[:, e * w : (e + 1) * w],
                     lhsT=wu_codes[u][:, e, :].bitcast(FP8X4),
-                    lhsT_scale=wu_plane[u][:, e, :],
+                    lhsT_scale=wu_scale[u][:, e, :],
                     rhs=u_codes[:, t0 : t0 + w].bitcast(FP8X4),
-                    rhs_scale=u_plane[:, t0 : t0 + w],
+                    rhs_scale=u_scale[:, t0 : t0 + w],
                     start=True,
                     stop=True,
                 )
@@ -121,95 +128,96 @@ def tile_moe_prv_lin_none_kernel(tc, uT, wu, w_words, w_scales, gate, offs, pos1
             nc.scalar.copy(**wu_views(1, h))
         wu_quantize(0)
         wu_quantize(1)
-        nc.vector.tensor_copy(**u_views(0, 0, 160))
-        nc.scalar.copy(**u_views(0, 160, 256))
+        nc.vector.tensor_copy(**u_views(0, 0, FIRST_GROUP_ON_VECTOR))
+        nc.scalar.copy(**u_views(0, FIRST_GROUP_ON_VECTOR, 256))
         u_quantize(0)
-        nc.vector.tensor_copy(**u_views(1, 0, 128))
-        nc.scalar.copy(**u_views(2, 0, 128))
+        nc.vector.tensor_copy(**u_views(1, 0, P))
+        nc.scalar.copy(**u_views(2, 0, P))
         u_quantize(1)
-        nc.vector.tensor_copy(**u_views(3, 0, 96))
-        nc.scalar.copy(**u_views(3, 96, 128))
+        nc.vector.tensor_copy(**u_views(3, 0, LAST_GROUP_ON_VECTOR))
+        nc.scalar.copy(**u_views(3, LAST_GROUP_ON_VECTOR, P))
         u_quantize(2)
         u_quantize(3)
         nc.scalar.copy(**project(0, 0, 256, bank(0, "x0_a")[:]))
-        nc.vector.tensor_copy(**project(0, 256, 128, bank(1, "x0_b")[:, 0:256]))
-        nc.vector.tensor_copy(**project(0, 384, 128, bank(2, "x0_c")[:, 0:256]))
-        nc.scalar.copy(**project(0, 512, 128, bank(3, "x0_d")[:, 0:256]))
-        nc.scalar.copy(**project(1, 512, 128, bank(1, "x1_c")[:, 0:256]))
-        nc.scalar.copy(**project(1, 0, 256, bank(2, "x1_a")[:]))
-        nc.scalar.copy(**project(1, 256, 256, bank(3, "x1_b")[:]))
+        nc.vector.tensor_copy(**project(0, 256, P, bank(1, "x0_b")[:, 0:256]))
+        nc.vector.tensor_copy(**project(0, 384, P, bank(2, "x0_c")[:, 0:256]))
+        shared = bank(3, "x_shared")
+        early = project(1, 0, P, shared[:, 256:BANK])
+        nc.scalar.copy(**project(0, 512, P, shared[:, 0:256]))
+        nc.scalar.copy(**early)
+        nc.scalar.copy(**project(1, P, 256, bank(1, "x1_b")[:]))
+        nc.scalar.copy(**project(1, 384, 256, bank(2, "x1_c")[:]))
         x_single = keep.tile([P, 2, T], BF16, name="x_single")
-        for t0, t1, engine in ((0, 384, nc.vector), (384, T, nc.gpsimd)):
+        for t0, t1, engine in ((0, SINGLES_ON_VECTOR, nc.vector), (SINGLES_ON_VECTOR, T, nc.gpsimd)):
             engine.tensor_copy(out=x_single[:, :, t0:t1], in_=x_pairs[0][:, t0:t1, :].rearrange("p t e -> p e t"))
 
         xs_head = keep.tile([P, 2, SPLIT], U32, name="xs_head")
-        xs_tail = [keep.tile([P, 2, C], U32, name="xs_tail%d" % ex) for ex in range(2)]
+        xs_tail = [keep.tile([P, 2, C], U32, name="xs_tail%d" % ex) for ex in range(E - HEAD_EXPERTS)]
         xs_bf = keep.tile([P, S, 4], BF16, name="xs_bf", align_bytes=64)
         xs_codes = keep.tile([P, S], U32, name="xs_codes", align_bytes=64)
-        xs_plane = keep.tile([P, S], U8, name="xs_plane", align_bytes=64)
+        xs_scale = keep.tile([P, S], U8, name="xs_scale", align_bytes=64)
 
-        def planes(s0, n):
+        def gathered(s0, n):
             return xs_head[:, :, s0 : s0 + n] if s0 < SPLIT else xs_tail[(s0 - SPLIT) // C][:]
 
-        def gather_x(u, s0, n):
+        def gather_pair(u, s0, n):
             window = x_pairs[u][:].rearrange("p t e -> p (t e)").bitcast(U32)
-            nc.vector.tensor_copy(planes(s0, n)[:, u, :], window.indirect(offs_sb[:, s0 // 16 : (s0 + n) // 16]))
+            nc.vector.tensor_copy(gathered(s0, n)[:, u, :], window.indirect(offs_sb[:, s0 // 16 : (s0 + n) // 16]))
 
         def gather_single(e, s0, n):
-            halves = planes(s0, n)[:, 0, :].bitcast(BF16).rearrange("p (s e) -> p s e", e=2)
+            halves = gathered(s0, n)[:, 0, :].bitcast(BF16).rearrange("p (s e) -> p s e", e=2)
             nc.scalar.activation(halves[:, :, e], x_single[:, e, :].indirect(offs_sb[:, s0 // 16 : (s0 + n) // 16]), COPY)
 
         def interleave(s0, n):
             words = xs_bf[:].rearrange("p s j -> p (s j)").bitcast(U32).rearrange("p (s u) -> p s u", u=2)
-            return dict(out=words[:, s0 : s0 + n, :], in_=planes(s0, n).rearrange("p u s -> p s u"))
+            return dict(out=words[:, s0 : s0 + n, :], in_=gathered(s0, n).rearrange("p u s -> p s u"))
 
         def xs_quantize(s0, n):
             nc.vector.quantize_mx(
                 out=xs_codes[:, s0 : s0 + n].bitcast(FP8X4),
-                scales=xs_plane[:, s0 : s0 + n],
+                scales=xs_scale[:, s0 : s0 + n],
                 in_=xs_bf[:, s0 : s0 + n, :].rearrange("p s j -> p (s j)"),
             )
 
-        y_sb = [keep.tile([P, S], F32, name="y_sb%d" % i) for i in range(3)]
+        y_sb = [keep.tile([P, S], F32, name="y_sb%d" % i) for i in range(N // P)]
 
         def experts(i, s0, n, step, sums):
             for a in range(0, n, step):
-                e = (s0 + a) // C
+                ex = (s0 + a) // C
                 nc.tensor.matmul_mx(
                     out=sums[:, a : a + step],
-                    lhsT=w_codes[:, e, P * i : P * (i + 1)].bitcast(FP8X4),
-                    lhsT_scale=w_plane[:, e, P * i : P * (i + 1)],
+                    lhsT=w_codes[:, ex, P * i : P * (i + 1)].bitcast(FP8X4),
+                    lhsT_scale=w_scale[:, ex, P * i : P * (i + 1)],
                     rhs=xs_codes[:, s0 + a : s0 + a + step].bitcast(FP8X4),
-                    rhs_scale=xs_plane[:, s0 + a : s0 + a + step],
+                    rhs_scale=xs_scale[:, s0 + a : s0 + a + step],
                     start=True,
                     stop=True,
                 )
             return dict(out=y_sb[i][:, s0 : s0 + n], in_=sums)
 
-        gather_x(0, 0, 384)
-        gather_x(0, 384, 384)
-        for ex in (3, 4):
+        gather_pair(0, 0, SPLIT // 2)
+        gather_pair(0, SPLIT // 2, SPLIT // 2)
+        for ex in range(HEAD_EXPERTS, E):
             for e in range(2):
                 gather_single(e, ex * C, C)
         for ex in range(E):
-            gather_x(1, ex * C, C)
-            if ex < 3:
-                nc.gpsimd.tensor_copy(**interleave(ex * C, C))
-            else:
-                nc.scalar.copy(**interleave(ex * C, C))
+            gather_pair(1, ex * C, C)
+            cut = min(max(ON_GPSIMD, ex * C), (ex + 1) * C)
+            if cut > ex * C:
+                nc.gpsimd.tensor_copy(**interleave(ex * C, cut - ex * C))
+            if cut < (ex + 1) * C:
+                nc.scalar.copy(**interleave(cut, (ex + 1) * C - cut))
         for s0, n in SLOT_GROUPS:
             xs_quantize(s0, n)
-        nc.scalar.copy(**experts(0, 0, 512, C, bank(0, "y0_0")[:]))
-        for e in range(2, 4):
-            nc.vector.tensor_copy(**experts(0, e * C, C, C, bank(e, "y0_%d" % e)[:, 0:C]))
-        nc.scalar.copy(**experts(0, 1024, P, P, bank(4, "y0_4")[:, 0:P]))
-        nc.scalar.copy(**experts(0, 1152, P, P, bank(5, "y0_5")[:, 0:P]))
-        nc.scalar.copy(**experts(1, 0, 512, C, bank(4, "y1_a")[:]))
-        nc.scalar.copy(**experts(1, 512, 512, C, bank(5, "y1_b")[:]))
-        nc.scalar.copy(**experts(1, 1024, C, C, bank(3, "y1_c")[:, 0:C]))
-        nc.scalar.copy(**experts(2, 0, 512, C, bank(3, "y2_a")[:]))
-        nc.scalar.copy(**experts(2, 512, 512, C, bank(4, "y2_b")[:]))
-        nc.scalar.copy(**experts(2, 1024, C, C, bank(5, "y2_c")[:, 0:C]))
+        nc.scalar.copy(**experts(0, 0, 2 * C, C, bank(0, "y0_0")[:]))
+        for ex in (2, 3):
+            nc.vector.tensor_copy(**experts(0, ex * C, C, C, bank(ex, "y0_%d" % ex)[:, 0:C]))
+        nc.scalar.copy(**experts(0, 4 * C, P, P, bank(4, "y0_4")[:, 0:P]))
+        nc.scalar.copy(**experts(0, 4 * C + P, P, P, bank(5, "y0_5")[:, 0:P]))
+        for i, banks in ((1, (4, 5, 3)), (2, (3, 4, 5))):
+            for s0, b in zip(range(0, S, BANK), banks):
+                n = min(BANK, S - s0)
+                nc.scalar.copy(**experts(i, s0, n, C, bank(b, "y%d_%d" % (i, s0))[:, 0:n]))
 
         o_sb = [keep.tile([P, T], F32, name="o_sb%d" % i) for i in range(2)]
         lists = (pos1_sb, pos2_sb)
@@ -223,7 +231,7 @@ def tile_moe_prv_lin_none_kernel(tc, uT, wu, w_words, w_scales, gate, offs, pos1
                 fetch(i, r, t0, t1, terms[r][:])
             return terms
 
-        def add_in_psum(i, t0, t1, terms, banks):
+        def add_in_psum(i, t0, t1, terms, banks, queue):
             there = bank(banks[0], "there%d_%d" % (i, t0))
             back = bank(banks[1], "back%d_%d" % (i, t0))
             turned = keep.tile([P, t1 - t0], F32, name="turned%d_%d" % (i, t0), tag="turned%d_%d" % (i, t0))
@@ -241,27 +249,28 @@ def tile_moe_prv_lin_none_kernel(tc, uT, wu, w_words, w_scales, gate, offs, pos1
             for t in range(t0, t1, P):
                 nc.tensor.transpose(back[:, t - t0 : t - t0 + P], turned[:, t - t0 : t - t0 + P], ident[:])
             nc.scalar.copy(out=o_sb[i][:, t0:t1], in_=back[:, 0 : t1 - t0])
-            (nc.sync, nc.scalar)[i].dma_start(out=out[P * i : P * (i + 1), t0:t1], in_=o_sb[i][:, t0:t1])
+            queue.dma_start(out=out[P * i : P * (i + 1), t0:t1], in_=o_sb[i][:, t0:t1])
 
-        def add_on_vector(t0, t1, total, first, second):
-            nc.vector.tensor_tensor(total, first, second, ADD)
+        def add_on_vector(t0, t1, total, term0, term1):
+            nc.vector.tensor_tensor(total, term0, term1, ADD)
             nc.sync.dma_start(out=out[2 * P : 3 * P, t0:t1], in_=total)
 
         whole = fetch_both(0, 0, T)
-        add_in_psum(0, 0, 384, [term[:, 0:384] for term in whole], (0, 1))
-        add_in_psum(0, 384, T, [term[:, 384:T] for term in whole], (6, 7))
-        add_in_psum(1, 0, 384, fetch_both(1, 0, 384), (0, 2))
-        add_in_psum(1, 384, T, fetch_both(1, 384, T), (6, 4))
+        add_in_psum(0, 0, CUT, [term[:, 0:CUT] for term in whole], (0, 1), nc.sync)
+        add_in_psum(0, CUT, T, [term[:, CUT:T] for term in whole], (6, 7), nc.sync)
+        add_in_psum(1, 0, CUT, fetch_both(1, 0, CUT), (0, 2), nc.scalar)
+        add_in_psum(1, CUT, T, fetch_both(1, CUT, T), (6, 4), nc.scalar)
 
-        first = keep.tile([P, T], F32, name="first")
-        second = keep.tile([P, 512], F32, name="second")
-        fetch(2, 0, 0, T, first[:])
-        fetch(2, 1, 0, 384, second[:, 0:384])
-        fetch(2, 1, 384, 512, second[:, 384:512])
-        o_head = keep.tile([P, 384], F32, name="o_head", tag="term11_0")
-        add_on_vector(0, 384, o_head[:], first[:, 0:384], second[:, 0:384])
-        second_end = keep.tile([P, P], F32, name="second_end", tag="term11_384")
-        fetch(2, 1, 512, T, second_end[:])
-        o_tail = keep.tile([P, 256], F32, name="o_tail", tag="turned1_384")
-        add_on_vector(384, 512, o_tail[:, 0:P], first[:, 384:512], second[:, 384:512])
-        add_on_vector(512, T, o_tail[:, P : 2 * P], first[:, 512:T], second_end[:])
+        last = T - P
+        first_term = keep.tile([P, T], F32, name="first_term")
+        second_term = keep.tile([P, last], F32, name="second_term")
+        fetch(2, 0, 0, T, first_term[:])
+        fetch(2, 1, 0, CUT, second_term[:, 0:CUT])
+        fetch(2, 1, CUT, last, second_term[:, CUT:last])
+        o_head = keep.tile([P, CUT], F32, name="o_head", tag="term11_0")
+        add_on_vector(0, CUT, o_head[:], first_term[:, 0:CUT], second_term[:, 0:CUT])
+        second_end = keep.tile([P, P], F32, name="second_end", tag="term11_%d" % CUT)
+        fetch(2, 1, last, T, second_end[:])
+        o_tail = keep.tile([P, T - CUT], F32, name="o_tail", tag="turned1_%d" % CUT)
+        add_on_vector(CUT, last, o_tail[:, 0:P], first_term[:, CUT:last], second_term[:, CUT:last])
+        add_on_vector(last, T, o_tail[:, P : 2 * P], first_term[:, last:T], second_end[:])

@@ -72,6 +72,9 @@ def tile_moe_prv_lin_none_kernel(tc, uT, wu, w_words, w_scales, gate, offs, pos1
         nc.sync.dma_start(pos2_sb[:], pos2)
         gate_sb = keep.tile([P, 2, T], F32, name="gate_sb")
         nc.sync.dma_start(out=gate_sb[:], in_=gate[:, 0:P, :].rearrange("r p t -> p r t"))
+        gate_col = keep.tile([P, T // P], F32, name="gate_col")
+        with nc.allow_non_contiguous_dma(reason="one weight a partition"):
+            nc.sync.dma_start(out=gate_col[:], in_=gate[0, 0, :].rearrange("(b p) -> p b", p=P))
 
         x_pairs = [keep.tile([P, T, 2], BF16, name="x_pairs%d" % u, tag=("u_raw2", "x_pairs1")[u], align_bytes=(32, 64)[u]) for u in range(2)]
         wu_bf = [keep.tile([P, 2, P, 4], BF16, name="wu_bf%d" % u, align_bytes=64) for u in range(2)]
@@ -214,63 +217,63 @@ def tile_moe_prv_lin_none_kernel(tc, uT, wu, w_words, w_scales, gate, offs, pos1
             nc.vector.tensor_copy(**experts(0, ex * C, C, C, bank(ex, "y0_%d" % ex)[:, 0:C]))
         nc.scalar.copy(**experts(0, 4 * C, P, P, bank(4, "y0_4")[:, 0:P]))
         nc.scalar.copy(**experts(0, 4 * C + P, P, P, bank(5, "y0_5")[:, 0:P]))
-        for i, banks in ((1, (4, 5, 3)), (2, (3, 4, 5))):
+        def row_tile(i, banks):
             for s0, b in zip(range(0, S, BANK), banks):
                 n = min(BANK, S - s0)
                 nc.scalar.copy(**experts(i, s0, n, C, bank(b, "y%d_%d" % (i, s0))[:, 0:n]))
 
-        o_sb = [keep.tile([P, T], F32, name="o_sb%d" % i) for i in range(2)]
+        row_tile(1, (1, 6, 7))
+
         lists = (pos1_sb, pos2_sb)
 
-        def fetch(i, r, t0, t1, term):
-            nc.vector.tensor_tensor(term, y_sb[i][:].indirect(lists[r][:, t0 // 16 : t1 // 16]), gate_sb[:, r, t0:t1], MULT)
+        def fetch(i, r, t0, t1, tag=None):
+            name = "term%d%d_%d" % (i, r, t0)
+            term = keep.tile([P, t1 - t0], F32, name=name, tag=tag or name)
+            nc.vector.tensor_tensor(term[:], y_sb[i][:].indirect(lists[r][:, t0 // 16 : t1 // 16]), gate_sb[:, r, t0:t1], MULT)
+            return term
 
-        def fetch_both(i, t0, t1):
-            terms = [keep.tile([P, t1 - t0], F32, name="term%d%d_%d" % (i, r, t0), tag="term%d%d_%d" % (i, r, t0)) for r in range(2)]
-            for r in range(2):
-                fetch(i, r, t0, t1, terms[r][:])
-            return terms
+        def fetch_plain(i, t0, t1, plain):
+            nc.scalar.activation(plain[:, t0:t1], y_sb[i][:].indirect(pos1_sb[:, t0 // 16 : t1 // 16]), COPY)
 
-        def add_in_psum(i, t0, t1, terms, banks, queue):
+        def weigh(i, t0, t1, plain, banks):
             there = bank(banks[0], "there%d_%d" % (i, t0))
             back = bank(banks[1], "back%d_%d" % (i, t0))
             turned = keep.tile([P, t1 - t0], F32, name="turned%d_%d" % (i, t0), tag="turned%d_%d" % (i, t0))
-            for r in range(2):
-                for t in range(t0, t1, P):
-                    nc.tensor.matmul(
-                        there[:, t - t0 : t - t0 + P],
-                        terms[r][:, t - t0 : t - t0 + P],
-                        ident[:],
-                        start=(r == 0 and t == t0),
-                        stop=(r == 1 and t == t1 - P),
-                        is_transpose=True,
-                    )
-            nc.scalar.copy(out=turned[:], in_=there[:, 0 : t1 - t0])
-            for t in range(t0, t1, P):
-                nc.tensor.transpose(back[:, t - t0 : t - t0 + P], turned[:, t - t0 : t - t0 + P], ident[:])
-            nc.scalar.copy(out=o_sb[i][:, t0:t1], in_=back[:, 0 : t1 - t0])
-            queue.dma_start(out=out[P * i : P * (i + 1), t0:t1], in_=o_sb[i][:, t0:t1])
+            blocks = [slice(t - t0, t - t0 + P) for t in range(t0, t1, P)]
+            for cols in blocks:
+                nc.tensor.transpose(there[:, cols], plain[:, cols], ident[:])
+            for b, cols in enumerate(blocks):
+                nc.scalar.activation(turned[:, cols], there[:, cols], COPY, scale=gate_col[:, t0 // P + b : t0 // P + b + 1])
+            for cols in blocks:
+                nc.tensor.transpose(back[:, cols], turned[:, cols], ident[:])
+            return back[:, 0 : t1 - t0]
 
-        def add_on_vector(t0, t1, total, term0, term1):
-            nc.vector.tensor_tensor(total, term0, term1, ADD)
-            nc.sync.dma_start(out=out[2 * P : 3 * P, t0:t1], in_=total)
+        def add_and_store(i, t0, t1, first, second, tag=None):
+            name = "total%d_%d" % (i, t0)
+            total = keep.tile([P, t1 - t0], F32, name=name, tag=tag or name)
+            nc.vector.tensor_tensor(total[:], first, second, ADD)
+            nc.sync.dma_start(out=out[P * i : P * (i + 1), t0:t1], in_=total[:])
 
-        whole = fetch_both(0, 0, T)
-        add_in_psum(0, 0, CUT, [term[:, 0:CUT] for term in whole], (0, 1), nc.sync)
-        add_in_psum(0, CUT, T, [term[:, CUT:T] for term in whole], (6, 7), nc.sync)
-        add_in_psum(1, 0, CUT, fetch_both(1, 0, CUT), (0, 2), nc.scalar)
-        add_in_psum(1, CUT, T, fetch_both(1, CUT, T), (6, 4), nc.scalar)
+        second = fetch(0, 1, 0, T)
+        first = [fetch(0, 0, 0, CUT), fetch(0, 0, CUT, T)]
+        add_and_store(0, 0, CUT, first[0][:], second[:, 0:CUT])
+        add_and_store(0, CUT, T, first[1][:], second[:, CUT:T])
 
         last = T - P
-        first_term = keep.tile([P, T], F32, name="first_term")
-        second_term = keep.tile([P, last], F32, name="second_term")
-        fetch(2, 0, 0, T, first_term[:])
-        fetch(2, 1, 0, CUT, second_term[:, 0:CUT])
-        fetch(2, 1, CUT, last, second_term[:, CUT:last])
-        o_head = keep.tile([P, CUT], F32, name="o_head", tag="term11_0")
-        add_on_vector(0, CUT, o_head[:], first_term[:, 0:CUT], second_term[:, 0:CUT])
-        second_end = keep.tile([P, P], F32, name="second_end", tag="term11_%d" % CUT)
-        fetch(2, 1, last, T, second_end[:])
-        o_tail = keep.tile([P, T - CUT], F32, name="o_tail", tag="turned1_%d" % CUT)
-        add_on_vector(CUT, last, o_tail[:, 0:P], first_term[:, CUT:last], second_term[:, CUT:last])
-        add_on_vector(last, T, o_tail[:, P : 2 * P], first_term[:, last:T], second_end[:])
+        plain = keep.tile([P, T], F32, name="plain1", tag="plain")
+        fetch_plain(1, 0, T, plain)
+        row_tile(2, (0, 2, 3))
+        weighed1 = [weigh(1, 0, CUT, plain[:, 0:CUT], (4, 1)), weigh(1, CUT, T, plain[:, CUT:T], (5, 6))]
+        plain = keep.tile([P, last], F32, name="plain2", tag="plain")
+        fetch_plain(2, 0, 2 * P, plain)
+        fetch_plain(2, 2 * P, last, plain)
+        weighed2 = [weigh(2, 0, 2 * P, plain[:, 0 : 2 * P], (7, 2)), weigh(2, 2 * P, last, plain[:, 2 * P : last], (0, 3))]
+        second1 = fetch(1, 1, 0, T)
+        first_end = fetch(2, 0, last, T)
+        second_lo = fetch(2, 1, 0, 2 * P)
+        add_and_store(1, 0, CUT, weighed1[0], second1[:, 0:CUT])
+        second_hi = fetch(2, 1, 2 * P, T, tag="turned1_0")
+        add_and_store(1, CUT, T, weighed1[1], second1[:, CUT:T])
+        add_and_store(2, 0, 2 * P, weighed2[0], second_lo[:])
+        add_and_store(2, last, T, first_end[:], second_hi[:, 2 * P : 3 * P], tag="turned2_0")
+        add_and_store(2, 2 * P, last, weighed2[1], second_hi[:, 0 : 2 * P])

@@ -264,16 +264,20 @@ def tile_moe_prv_lin_none_kernel(tc, uT, wu, w_words, w_scales, gate, offs, pos1
         fetch_plain(1, 0, T, plain)
         row_tile(2, (0, 2, 3))
         weighed1 = [weigh(1, 0, CUT, plain[:, 0:CUT], (4, 1)), weigh(1, CUT, T, plain[:, CUT:T], (5, 6))]
-        plain = keep.tile([P, last], F32, name="plain2", tag="plain")
+        plain = keep.tile([P, CUT], F32, name="plain2", tag="plain")
         fetch_plain(2, 0, 2 * P, plain)
-        fetch_plain(2, 2 * P, last, plain)
-        weighed2 = [weigh(2, 0, 2 * P, plain[:, 0 : 2 * P], (7, 2)), weigh(2, 2 * P, last, plain[:, 2 * P : last], (0, 3))]
+        fetch_plain(2, 2 * P, CUT, plain)
+        weighed2 = [weigh(2, 0, 2 * P, plain[:, 0 : 2 * P], (7, 2)), weigh(2, 2 * P, CUT, plain[:, 2 * P : CUT], (0, 3))]
         second1 = fetch(1, 1, 0, T)
-        first_end = fetch(2, 0, last, T)
+        first_mid = fetch(2, 0, CUT, last)
         second_lo = fetch(2, 1, 0, 2 * P)
         add_and_store(1, 0, CUT, weighed1[0], second1[:, 0:CUT])
-        second_hi = fetch(2, 1, 2 * P, T, tag="turned1_0")
         add_and_store(1, CUT, T, weighed1[1], second1[:, CUT:T])
+        second_hi = fetch(2, 1, 2 * P, T, tag="turned1_%d" % CUT)
         add_and_store(2, 0, 2 * P, weighed2[0], second_lo[:])
-        add_and_store(2, last, T, first_end[:], second_hi[:, 2 * P : 3 * P], tag="turned2_0")
-        add_and_store(2, 2 * P, last, weighed2[1], second_hi[:, 0 : 2 * P])
+        first_end = fetch(2, 0, last, T, tag="turned2_0")
+        add_and_store(2, 2 * P, CUT, weighed2[1], second_hi[:, 0:P])
+        ends = keep.tile([P, 2 * P], F32, name="ends", tag="turned2_%d" % (2 * P))
+        for k, first in enumerate((first_mid, first_end)):
+            nc.vector.tensor_tensor(ends[:, k * P : (k + 1) * P], first[:], second_hi[:, (k + 1) * P : (k + 2) * P], ADD)
+            nc.sync.dma_start(out=out[2 * P : 3 * P, CUT + k * P : CUT + (k + 1) * P], in_=ends[:, k * P : (k + 1) * P])

@@ -28,7 +28,7 @@ SINGLES_ON_VECTOR = 384
 HEAD_EXPERTS = 3
 SPLIT = HEAD_EXPERTS * C
 ON_GPSIMD = 2 * C + P
-SLOT_GROUPS = ((0, 2 * C), (2 * C, C), (3 * C, C), (4 * C, P), (4 * C + P, P))
+SLOT_GROUPS = ((0, C), (C, C), (2 * C, C), (3 * C, C), (4 * C, P), (4 * C + P, P))
 CUT = 384
 
 
@@ -154,10 +154,9 @@ def tile_moe_prv_lin_none_kernel(tc, uT, wu, w_words, w_scales, gate, offs, pos1
         for t0, t1, engine in ((0, SINGLES_ON_VECTOR, nc.vector), (SINGLES_ON_VECTOR, T, nc.gpsimd)):
             engine.tensor_copy(out=x_single[:, :, t0:t1], in_=x_pairs[0][:, t0:t1, :].rearrange("p t e -> p e t"))
 
-        xs_head = keep.tile([P, 2, SPLIT], U32, name="xs_head")
+        xs_head = keep.tile([P, 2, SPLIT], U32, name="xs_head", tag="xs_head", align_bytes=64)
         xs_tail = [keep.tile([P, 2, C], U32, name="xs_tail%d" % ex) for ex in range(E - HEAD_EXPERTS)]
         xs_bf = keep.tile([P, S, 4], BF16, name="xs_bf", align_bytes=64)
-        xs_codes = keep.tile([P, S], U32, name="xs_codes", align_bytes=64)
         xs_scale = keep.tile([P, S], U8, name="xs_scale", align_bytes=64)
 
         def gathered(s0, n):
@@ -210,74 +209,74 @@ def tile_moe_prv_lin_none_kernel(tc, uT, wu, w_words, w_scales, gate, offs, pos1
                 nc.gpsimd.tensor_copy(**interleave(ex * C, cut - ex * C))
             if cut < (ex + 1) * C:
                 nc.scalar.copy(**interleave(cut, (ex + 1) * C - cut))
+        xs_codes = keep.tile([P, S], U32, name="xs_codes", tag="xs_head", align_bytes=64)
         for s0, n in SLOT_GROUPS:
             xs_quantize(s0, n)
-        nc.scalar.copy(**experts(0, 0, 2 * C, C, bank(0, "y0_0")[:]))
+        for ex in (0, 1):
+            nc.scalar.copy(**experts(0, ex * C, C, C, bank(ex, "y0_%d" % ex)[:, 0:C]))
         for ex in (2, 3):
             nc.vector.tensor_copy(**experts(0, ex * C, C, C, bank(ex, "y0_%d" % ex)[:, 0:C]))
         nc.scalar.copy(**experts(0, 4 * C, P, P, bank(4, "y0_4")[:, 0:P]))
         nc.scalar.copy(**experts(0, 4 * C + P, P, P, bank(5, "y0_5")[:, 0:P]))
-        def row_tile(i, banks):
-            for s0, b in zip(range(0, S, BANK), banks):
-                n = min(BANK, S - s0)
-                nc.scalar.copy(**experts(i, s0, n, C, bank(b, "y%d_%d" % (i, s0))[:, 0:n]))
 
-        row_tile(1, (1, 6, 7))
+        def empty(i, s0, b):
+            n = min(BANK, S - s0)
+            nc.scalar.copy(**experts(i, s0, n, C, bank(b, "y%d_%d" % (i, s0))[:, 0:n]))
 
         lists = (pos1_sb, pos2_sb)
+        out_rows = out.rearrange("(i p) t -> p i t", p=P)
+        last = T // P - 1
+        second = keep.tile([P, 2, T], F32, name="second")
+        plain = keep.tile([P, 2, T], F32, name="plain")
 
-        def fetch(i, r, t0, t1, tag=None):
-            name = "term%d%d_%d" % (i, r, t0)
-            term = keep.tile([P, t1 - t0], F32, name=name, tag=tag or name)
-            nc.vector.tensor_tensor(term[:], y_sb[i][:].indirect(lists[r][:, t0 // 16 : t1 // 16]), gate_sb[:, r, t0:t1], MULT)
-            return term
+        def fetch(i, r, t0, t1, term):
+            nc.vector.tensor_tensor(term, y_sb[i][:].indirect(lists[r][:, t0 // 16 : t1 // 16]), gate_sb[:, r, t0:t1], MULT)
 
-        def fetch_plain(i, t0, t1, plain):
-            nc.scalar.activation(plain[:, t0:t1], y_sb[i][:].indirect(pos1_sb[:, t0 // 16 : t1 // 16]), COPY)
+        def fetch_plain(i, t0, t1):
+            nc.scalar.activation(plain[:, i - 1, t0:t1], y_sb[i][:].indirect(pos1_sb[:, t0 // 16 : t1 // 16]), COPY)
 
-        def weigh(i, t0, t1, plain, banks):
-            there = bank(banks[0], "there%d_%d" % (i, t0))
-            back = bank(banks[1], "back%d_%d" % (i, t0))
-            turned = keep.tile([P, t1 - t0], F32, name="turned%d_%d" % (i, t0), tag="turned%d_%d" % (i, t0))
-            blocks = [slice(t - t0, t - t0 + P) for t in range(t0, t1, P)]
-            for cols in blocks:
-                nc.tensor.transpose(there[:, cols], plain[:, cols], ident[:])
-            for b, cols in enumerate(blocks):
-                nc.scalar.activation(turned[:, cols], there[:, cols], COPY, scale=gate_col[:, t0 // P + b : t0 // P + b + 1])
-            for cols in blocks:
-                nc.tensor.transpose(back[:, cols], turned[:, cols], ident[:])
-            return back[:, 0 : t1 - t0]
+        def weigh(b, n, banks, turned):
+            there = bank(banks[0], "there%d" % b)[:, 0 : n * P]
+            back = bank(banks[1], "back%d" % b)[:, 0 : n * P]
+            for i in range(n):
+                nc.tensor.transpose(there[:, P * i : P * (i + 1)], plain[:, i, P * b : P * (b + 1)], ident[:])
+            nc.scalar.activation(turned, there, COPY, scale=gate_col[:, b : b + 1])
+            for i in range(n):
+                nc.tensor.transpose(back[:, P * i : P * (i + 1)], turned[:, P * i : P * (i + 1)], ident[:])
+            return back.rearrange("p (i t) -> p i t", i=n)
 
-        def add_and_store(i, t0, t1, first, second, tag=None):
-            name = "total%d_%d" % (i, t0)
-            total = keep.tile([P, t1 - t0], F32, name=name, tag=tag or name)
-            nc.vector.tensor_tensor(total[:], first, second, ADD)
-            nc.sync.dma_start(out=out[P * i : P * (i + 1), t0:t1], in_=total[:])
+        def add_and_store(i0, i1, t0, t1, first, other, tag=None):
+            name = "total%d_%d" % (i0, t0)
+            total = keep.tile([P, i1 - i0, t1 - t0], F32, name=name, tag=tag or name)
+            nc.vector.tensor_tensor(total[:], first, other, ADD)
+            nc.sync.dma_start(out=out_rows[:, i0:i1, t0:t1], in_=total[:])
 
-        second = fetch(0, 1, 0, T)
-        first = [fetch(0, 0, 0, CUT), fetch(0, 0, CUT, T)]
-        add_and_store(0, 0, CUT, first[0][:], second[:, 0:CUT])
-        add_and_store(0, CUT, T, first[1][:], second[:, CUT:T])
+        terms0 = keep.tile([P, 2, T], F32, name="terms0")
+        fetch(0, 1, 0, T, terms0[:, 1, :])
+        for t0, t1 in ((0, CUT), (CUT, T)):
+            fetch(0, 0, t0, t1, terms0[:, 0, t0:t1])
+        for t0, t1 in ((0, CUT), (CUT, T)):
+            add_and_store(0, 1, t0, t1, terms0[:, 0:1, t0:t1], terms0[:, 1:2, t0:t1])
 
-        last = T - P
-        plain = keep.tile([P, T], F32, name="plain1", tag="plain")
-        fetch_plain(1, 0, T, plain)
-        row_tile(2, (0, 2, 3))
-        weighed1 = [weigh(1, 0, CUT, plain[:, 0:CUT], (4, 1)), weigh(1, CUT, T, plain[:, CUT:T], (5, 6))]
-        plain = keep.tile([P, CUT], F32, name="plain2", tag="plain")
-        fetch_plain(2, 0, 2 * P, plain)
-        fetch_plain(2, 2 * P, CUT, plain)
-        weighed2 = [weigh(2, 0, 2 * P, plain[:, 0 : 2 * P], (7, 2)), weigh(2, 2 * P, CUT, plain[:, 2 * P : CUT], (0, 3))]
-        second1 = fetch(1, 1, 0, T)
-        first_mid = fetch(2, 0, CUT, last)
-        second_lo = fetch(2, 1, 0, 2 * P)
-        add_and_store(1, 0, CUT, weighed1[0], second1[:, 0:CUT])
-        add_and_store(1, CUT, T, weighed1[1], second1[:, CUT:T])
-        second_hi = fetch(2, 1, 2 * P, T, tag="turned1_%d" % CUT)
-        add_and_store(2, 0, 2 * P, weighed2[0], second_lo[:])
-        first_end = fetch(2, 0, last, T, tag="turned2_0")
-        add_and_store(2, 2 * P, CUT, weighed2[1], second_hi[:, 0:P])
-        ends = keep.tile([P, 2 * P], F32, name="ends", tag="turned2_%d" % (2 * P))
-        for k, first in enumerate((first_mid, first_end)):
-            nc.vector.tensor_tensor(ends[:, k * P : (k + 1) * P], first[:], second_hi[:, (k + 1) * P : (k + 2) * P], ADD)
-            nc.sync.dma_start(out=out[2 * P : 3 * P, CUT + k * P : CUT + (k + 1) * P], in_=ends[:, k * P : (k + 1) * P])
+        for s0, b in ((0, 1), (BANK, 6), (2 * BANK, 7)):
+            empty(1, s0, b)
+        empty(2, 0, 0)
+        fetch_plain(1, 0, T)
+        empty(2, BANK, 2)
+        empty(2, 2 * BANK, 3)
+        turned = keep.tile([P, T // P, 2 * P], F32, name="turned")
+        fetch(1, 1, 0, T, second[:, 0, :])
+        weighed = {last: weigh(last, 1, (4, 5), turned[:, last, 0:P])}
+        fetch_plain(2, 0, 2 * P)
+        fetch_plain(2, 2 * P, last * P)
+        for b, banks in enumerate(((6, 4), (7, 2), (0, 3), (1, 6))):
+            weighed[b] = weigh(b, 2, banks, turned[:, b, :])
+        fetch(2, 1, 0, T, second[:, 1, :])
+        first_end = keep.tile([P, 1, P], F32, name="first_end")
+        fetch(2, 0, last * P, T, first_end[:, 0, :])
+        add_and_store(1, 2, last * P, T, weighed[last], second[:, 0:1, last * P : T])
+        add_and_store(2, 3, last * P, T, first_end[:], second[:, 1:2, last * P : T])
+        for b in range(last - 1):
+            add_and_store(1, 3, P * b, P * (b + 1), weighed[b], second[:, :, P * b : P * (b + 1)])
+        for i in (1, 2):
+            add_and_store(i, i + 1, (last - 1) * P, last * P, weighed[last - 1][:, i - 1 : i, :], second[:, i - 1 : i, (last - 1) * P : last * P])

@@ -219,8 +219,7 @@ def tile_moe_prv_lin_none_kernel(tc, uT, wu, w_words, w_scales, gate, offs, pos1
         nc.scalar.copy(**experts(0, 4 * C, P, P, bank(4, "y0_4")[:, 0:P]))
         nc.scalar.copy(**experts(0, 4 * C + P, P, P, bank(5, "y0_5")[:, 0:P]))
 
-        def empty(i, s0, b):
-            n = min(BANK, S - s0)
+        def empty(i, s0, n, b):
             nc.scalar.copy(**experts(i, s0, n, C, bank(b, "y%d_%d" % (i, s0))[:, 0:n]))
 
         lists = (pos1_sb, pos2_sb)
@@ -258,12 +257,12 @@ def tile_moe_prv_lin_none_kernel(tc, uT, wu, w_words, w_scales, gate, offs, pos1
         for t0, t1 in ((0, CUT), (CUT, T)):
             add_and_store(0, 1, t0, t1, terms0[:, 0:1, t0:t1], terms0[:, 1:2, t0:t1])
 
-        for s0, b in ((0, 1), (BANK, 6), (2 * BANK, 7)):
-            empty(1, s0, b)
-        empty(2, 0, 0)
+        for s0, n, b in ((0, C, 1), (C, BANK, 6), (C + BANK, BANK, 7)):
+            empty(1, s0, n, b)
+        empty(2, 0, BANK, 0)
         fetch_plain(1, 0, T)
-        empty(2, BANK, 2)
-        empty(2, 2 * BANK, 3)
+        empty(2, BANK, BANK, 2)
+        empty(2, 2 * BANK, C, 3)
         turned = keep.tile([P, T // P, 2 * P], F32, name="turned")
         fetch(1, 1, 0, T, second[:, 0, :])
         weighed = {last: weigh(last, 1, (4, 5), turned[:, last, 0:P])}

@@ -244,10 +244,9 @@ def tile_moe_prv_lin_none_kernel(tc, uT, wu, w_words, w_scales, gate, offs, pos1
                 nc.tensor.transpose(back[:, P * i : P * (i + 1)], turned[:, P * i : P * (i + 1)], ident[:])
             return back.rearrange("p (i t) -> p i t", i=n)
 
-        def add_and_store(i0, i1, t0, t1, first, other, tag=None):
-            name = "total%d_%d" % (i0, t0)
-            total = keep.tile([P, i1 - i0, t1 - t0], F32, name=name, tag=tag or name)
-            nc.vector.tensor_tensor(total[:], first, other, ADD)
+        def add_and_store(i0, i1, t0, t1, first, other, engine=nc.vector):
+            total = keep.tile([P, i1 - i0, t1 - t0], F32, name="total%d_%d" % (i0, t0))
+            engine.tensor_tensor(total[:], first, other, ADD)
             nc.sync.dma_start(out=out_rows[:, i0:i1, t0:t1], in_=total[:])
 
         terms0 = keep.tile([P, 2, T], F32, name="terms0")
@@ -274,8 +273,9 @@ def tile_moe_prv_lin_none_kernel(tc, uT, wu, w_words, w_scales, gate, offs, pos1
         first_end = keep.tile([P, 1, P], F32, name="first_end")
         fetch(2, 0, last * P, T, first_end[:, 0, :])
         add_and_store(1, 2, last * P, T, weighed[last], second[:, 0:1, last * P : T])
-        add_and_store(2, 3, last * P, T, first_end[:], second[:, 1:2, last * P : T])
         for b in range(last - 1):
             add_and_store(1, 3, P * b, P * (b + 1), weighed[b], second[:, :, P * b : P * (b + 1)])
+            if b == 0:
+                add_and_store(2, 3, last * P, T, first_end[:], second[:, 1:2, last * P : T], nc.gpsimd)
         for i in (1, 2):
             add_and_store(i, i + 1, (last - 1) * P, last * P, weighed[last - 1][:, i - 1 : i, :], second[:, i - 1 : i, (last - 1) * P : last * P])

@@ -22,12 +22,12 @@ P = 128
 BANK = 512
 LOAD_WIDTH = 256
 TOKEN_LOADS = ((0, LOAD_WIDTH), (256, LOAD_WIDTH), (512, 128))
-TOKEN_GROUPS = ((0, 256), (256, 128), (384, 128), (512, 128))
-FIRST_GROUP_ON_VECTOR, LAST_GROUP_ON_VECTOR = 160, 96
+TOKEN_GROUPS = tuple((t0, 128) for t0 in range(0, T, 128))
+LAST_GROUP_ON_VECTOR = 96
 SINGLES_ON_VECTOR = 384
-HEAD_EXPERTS = 3
-SPLIT = HEAD_EXPERTS * C
-ON_GPSIMD = 2 * C + P
+SPLIT = 640
+HEAD_PIECES = ((0, C), (C, C), (2 * C, P))
+TAIL_PIECES = ((SPLIT, C + P), (4 * C, C))
 SLOT_GROUPS = ((0, C), (C, C), (2 * C, C), (3 * C, C), (4 * C, P), (4 * C + P, P))
 CUT = 384
 
@@ -113,54 +113,56 @@ def tile_moe_prv_lin_none_kernel(tc, uT, wu, w_words, w_scales, gate, offs, pos1
                 in_=u_bf[c][:].rearrange("p w j -> p (w j)"),
             )
 
-        def project(u, t0, w, sums):
-            for e in range(2):
-                nc.tensor.matmul_mx(
-                    out=sums[:, e * w : (e + 1) * w],
-                    lhsT=wu_codes[u][:, e, :].bitcast(FP8X4),
-                    lhsT_scale=wu_scale[u][:, e, :],
-                    rhs=u_codes[:, t0 : t0 + w].bitcast(FP8X4),
-                    rhs_scale=u_scale[:, t0 : t0 + w],
-                    start=True,
-                    stop=True,
-                )
-            return dict(out=x_pairs[u][:, t0 : t0 + w, :], in_=sums.rearrange("p (e t) -> p t e", e=2))
+        def project(u, groups, sums):
+            for n, c in enumerate(groups):
+                for e in range(2):
+                    nc.tensor.matmul_mx(
+                        out=sums[:, (2 * n + e) * P : (2 * n + e + 1) * P],
+                        lhsT=wu_codes[u][:, e, :].bitcast(FP8X4),
+                        lhsT_scale=wu_scale[u][:, e, :],
+                        rhs=u_codes[:, P * c : P * (c + 1)].bitcast(FP8X4),
+                        rhs_scale=u_scale[:, P * c : P * (c + 1)],
+                        start=True,
+                        stop=True,
+                    )
+            by_group = x_pairs[u][:].rearrange("p (c t) e -> p c t e", t=P)
+            return dict(out=by_group[:, slice(groups.start, groups.stop, groups.step), :, :], in_=sums.rearrange("p (c e t) -> p c t e", e=2, t=P))
 
         for h in range(2):
             nc.vector.tensor_copy(**wu_views(0, h))
             nc.scalar.copy(**wu_views(1, h))
         wu_quantize(0)
         wu_quantize(1)
-        nc.vector.tensor_copy(**u_views(0, 0, FIRST_GROUP_ON_VECTOR))
-        nc.scalar.copy(**u_views(0, FIRST_GROUP_ON_VECTOR, 256))
-        u_quantize(0)
-        nc.vector.tensor_copy(**u_views(1, 0, P))
-        nc.scalar.copy(**u_views(2, 0, P))
-        u_quantize(1)
-        nc.vector.tensor_copy(**u_views(3, 0, LAST_GROUP_ON_VECTOR))
-        nc.scalar.copy(**u_views(3, LAST_GROUP_ON_VECTOR, P))
-        u_quantize(2)
+        for c in (0, 2):
+            nc.vector.tensor_copy(**u_views(c, 0, P))
+            nc.scalar.copy(**u_views(c + 1, 0, P))
+            u_quantize(c)
+            if c == 0:
+                u_quantize(1)
+        nc.vector.tensor_copy(**u_views(4, 0, LAST_GROUP_ON_VECTOR))
+        nc.scalar.copy(**u_views(4, LAST_GROUP_ON_VECTOR, P))
         u_quantize(3)
-        nc.scalar.copy(**project(0, 0, 256, bank(0, "x0_a")[:]))
-        nc.vector.tensor_copy(**project(0, 256, P, bank(1, "x0_b")[:, 0:256]))
-        nc.vector.tensor_copy(**project(0, 384, P, bank(2, "x0_c")[:, 0:256]))
-        shared = bank(3, "x_shared")
-        early = project(1, 0, P, shared[:, 256:BANK])
-        nc.scalar.copy(**project(0, 512, P, shared[:, 0:256]))
+        u_quantize(4)
+        nc.scalar.copy(**project(0, range(0, 2), bank(0, "x0_a")[:]))
+        shared = [bank(3, "x_shared0"), bank(4, "x_shared1")]
+        early = project(1, range(0, 1), shared[0][:, 256:BANK])
+        nc.vector.tensor_copy(**project(0, range(2, 3), bank(1, "x0_b")[:, 0:256]))
+        nc.vector.tensor_copy(**project(0, range(3, 4), bank(2, "x0_c")[:, 0:256]))
+        nc.scalar.copy(**project(0, range(4, 5), shared[0][:, 0:256]))
         nc.scalar.copy(**early)
-        nc.scalar.copy(**project(1, P, 256, bank(1, "x1_b")[:]))
-        nc.scalar.copy(**project(1, 384, 256, bank(2, "x1_c")[:]))
+        nc.scalar.copy(**project(1, range(1, 5, 3), shared[1][:]))
+        nc.scalar.copy(**project(1, range(2, 4), bank(1, "x1_b")[:]))
         x_single = keep.tile([P, 2, T], BF16, name="x_single")
         for t0, t1, engine in ((0, SINGLES_ON_VECTOR, nc.vector), (SINGLES_ON_VECTOR, T, nc.gpsimd)):
             engine.tensor_copy(out=x_single[:, :, t0:t1], in_=x_pairs[0][:, t0:t1, :].rearrange("p t e -> p e t"))
 
         xs_head = keep.tile([P, 2, SPLIT], U32, name="xs_head", tag="xs_head", align_bytes=64)
-        xs_tail = [keep.tile([P, 2, C], U32, name="xs_tail%d" % ex) for ex in range(E - HEAD_EXPERTS)]
+        xs_tail = {s0: keep.tile([P, 2 * n], U32, name="xs_tail%d" % s0) for s0, n in TAIL_PIECES}
         xs_bf = keep.tile([P, S, 4], BF16, name="xs_bf", align_bytes=64)
         xs_scale = keep.tile([P, S], U8, name="xs_scale", align_bytes=64)
 
         def gathered(s0, n):
-            return xs_head[:, :, s0 : s0 + n] if s0 < SPLIT else xs_tail[(s0 - SPLIT) // C][:]
+            return xs_head[:, :, s0 : s0 + n] if s0 < SPLIT else xs_tail[s0][:].rearrange("p (u s) -> p u s", u=2)
 
         def gather_pair(u, s0, n):
             window = x_pairs[u][:].rearrange("p t e -> p (t e)").bitcast(U32)
@@ -170,9 +172,9 @@ def tile_moe_prv_lin_none_kernel(tc, uT, wu, w_words, w_scales, gate, offs, pos1
             halves = gathered(s0, n)[:, 0, :].bitcast(BF16).rearrange("p (s e) -> p s e", e=2)
             nc.scalar.activation(halves[:, :, e], x_single[:, e, :].indirect(offs_sb[:, s0 // 16 : (s0 + n) // 16]), COPY)
 
-        def interleave(s0, n):
+        def interleave(s0, n, a, b):
             words = xs_bf[:].rearrange("p s j -> p (s j)").bitcast(U32).rearrange("p (s u) -> p s u", u=2)
-            return dict(out=words[:, s0 : s0 + n, :], in_=gathered(s0, n).rearrange("p u s -> p s u"))
+            return dict(out=words[:, s0 + a : s0 + b, :], in_=gathered(s0, n).rearrange("p u s -> p s u")[:, a:b, :])
 
         def xs_quantize(s0, n):
             nc.vector.quantize_mx(
@@ -199,16 +201,16 @@ def tile_moe_prv_lin_none_kernel(tc, uT, wu, w_words, w_scales, gate, offs, pos1
 
         gather_pair(0, 0, SPLIT // 2)
         gather_pair(0, SPLIT // 2, SPLIT // 2)
-        for ex in range(HEAD_EXPERTS, E):
+        for s0, n in TAIL_PIECES:
             for e in range(2):
-                gather_single(e, ex * C, C)
-        for ex in range(E):
-            gather_pair(1, ex * C, C)
-            cut = min(max(ON_GPSIMD, ex * C), (ex + 1) * C)
-            if cut > ex * C:
-                nc.gpsimd.tensor_copy(**interleave(ex * C, cut - ex * C))
-            if cut < (ex + 1) * C:
-                nc.scalar.copy(**interleave(cut, (ex + 1) * C - cut))
+                gather_single(e, s0, n)
+        for s0, n in HEAD_PIECES:
+            gather_pair(1, s0, n)
+            nc.gpsimd.tensor_copy(**interleave(s0, n, 0, n))
+        for s0, n in TAIL_PIECES:
+            gather_pair(1, s0, n)
+            for a, b in ((0, P), (P, n)):
+                nc.scalar.copy(**interleave(s0, n, a, b))
         xs_codes = keep.tile([P, S], U32, name="xs_codes", tag="xs_head", align_bytes=64)
         for s0, n in SLOT_GROUPS:
             xs_quantize(s0, n)

@@ -24,9 +24,9 @@ LOAD_WIDTH = 256
 TOKEN_LOADS = ((0, LOAD_WIDTH), (256, LOAD_WIDTH), (512, 128))
 TOKEN_GROUPS = tuple((t0, 128) for t0 in range(0, T, 128))
 LAST_GROUP_ON_VECTOR = 96
-SINGLES_ON_VECTOR = 384
+SINGLES_ON_VECTOR = 192
 SPLIT = 640
-HEAD_PIECES = ((0, C), (C, C), (2 * C, P))
+HEAD_PIECES = ((0, P), (P, C), (P + C, C))
 TAIL_PIECES = ((SPLIT, C + P), (4 * C, C))
 SLOT_GROUPS = ((0, C), (C, C), (2 * C, C), (3 * C, C), (4 * C, P), (4 * C + P, P))
 CUT = 384
@@ -76,7 +76,8 @@ def tile_moe_prv_lin_none_kernel(tc, uT, wu, w_words, w_scales, gate, offs, pos1
         with nc.allow_non_contiguous_dma(reason="one weight a partition"):
             nc.sync.dma_start(out=gate_col[:], in_=gate[0, 0, :].rearrange("(b p) -> p b", p=P))
 
-        x_pairs = [keep.tile([P, T, 2], BF16, name="x_pairs%d" % u, tag=("u_raw2", "x_pairs1")[u], align_bytes=(32, 64)[u]) for u in range(2)]
+        x_all = keep.tile([P, 4 * T], BF16, name="x_all", tag="u_raw2", align_bytes=32)
+        x_pairs = [x_all[:, 2 * T * u : 2 * T * (u + 1)].rearrange("p (t e) -> p t e", e=2) for u in range(2)]
         wu_bf = [keep.tile([P, 2, P, 4], BF16, name="wu_bf%d" % u, align_bytes=64) for u in range(2)]
         wu_codes = [keep.tile([P, 2, P], U32, name="wu_codes%d" % u, align_bytes=64) for u in range(2)]
         wu_scale = [keep.tile([P, 2, P], U8, name="wu_scale%d" % u, align_bytes=64) for u in range(2)]
@@ -125,7 +126,7 @@ def tile_moe_prv_lin_none_kernel(tc, uT, wu, w_words, w_scales, gate, offs, pos1
                         start=True,
                         stop=True,
                     )
-            by_group = x_pairs[u][:].rearrange("p (c t) e -> p c t e", t=P)
+            by_group = x_pairs[u].rearrange("p (c t) e -> p c t e", t=P)
             return dict(out=by_group[:, slice(groups.start, groups.stop, groups.step), :, :], in_=sums.rearrange("p (c e t) -> p c t e", e=2, t=P))
 
         for h in range(2):
@@ -145,16 +146,16 @@ def tile_moe_prv_lin_none_kernel(tc, uT, wu, w_words, w_scales, gate, offs, pos1
         u_quantize(4)
         nc.scalar.copy(**project(0, range(0, 2), bank(0, "x0_a")[:]))
         shared = [bank(3, "x_shared0"), bank(4, "x_shared1")]
-        early = project(1, range(0, 1), shared[0][:, 256:BANK])
+        nc.vector.tensor_copy(**project(1, range(0, 1), bank(5, "x1_a")[:, 0:256]))
         nc.vector.tensor_copy(**project(0, range(2, 3), bank(1, "x0_b")[:, 0:256]))
         nc.vector.tensor_copy(**project(0, range(3, 4), bank(2, "x0_c")[:, 0:256]))
         nc.scalar.copy(**project(0, range(4, 5), shared[0][:, 0:256]))
-        nc.scalar.copy(**early)
         nc.scalar.copy(**project(1, range(1, 5, 3), shared[1][:]))
         nc.scalar.copy(**project(1, range(2, 4), bank(1, "x1_b")[:]))
         x_single = keep.tile([P, 2, T], BF16, name="x_single")
-        for t0, t1, engine in ((0, SINGLES_ON_VECTOR, nc.vector), (SINGLES_ON_VECTOR, T, nc.gpsimd)):
-            engine.tensor_copy(out=x_single[:, :, t0:t1], in_=x_pairs[0][:, t0:t1, :].rearrange("p t e -> p e t"))
+        nc.vector.tensor_copy(out=x_single[:, :, 0:SINGLES_ON_VECTOR], in_=x_pairs[0][:, 0:SINGLES_ON_VECTOR, :].rearrange("p t e -> p e t"))
+        for e in range(2):
+            nc.gpsimd.tensor_copy(out=x_single[:, e, SINGLES_ON_VECTOR:T], in_=x_pairs[0][:, SINGLES_ON_VECTOR:T, e])
 
         xs_head = keep.tile([P, 2, SPLIT], U32, name="xs_head", tag="xs_head", align_bytes=64)
         xs_tail = {s0: keep.tile([P, 2 * n], U32, name="xs_tail%d" % s0) for s0, n in TAIL_PIECES}
@@ -164,8 +165,8 @@ def tile_moe_prv_lin_none_kernel(tc, uT, wu, w_words, w_scales, gate, offs, pos1
         def gathered(s0, n):
             return xs_head[:, :, s0 : s0 + n] if s0 < SPLIT else xs_tail[s0][:].rearrange("p (u s) -> p u s", u=2)
 
-        def gather_pair(u, s0, n):
-            window = x_pairs[u][:].rearrange("p t e -> p (t e)").bitcast(U32)
+        def gather_pair(u, s0, n, spare=0):
+            window = x_all[:, 2 * T * u : 2 * (T * (u + 1) + spare)].bitcast(U32)
             nc.vector.tensor_copy(gathered(s0, n)[:, u, :], window.indirect(offs_sb[:, s0 // 16 : (s0 + n) // 16]))
 
         def gather_single(e, s0, n):
@@ -199,12 +200,13 @@ def tile_moe_prv_lin_none_kernel(tc, uT, wu, w_words, w_scales, gate, offs, pos1
                 )
             return dict(out=y_sb[i][:, s0 : s0 + n], in_=sums)
 
-        gather_pair(0, 0, SPLIT // 2)
-        gather_pair(0, SPLIT // 2, SPLIT // 2)
+        gather_pair(0, 0, 2 * C, 64)
         for s0, n in TAIL_PIECES:
             for e in range(2):
                 gather_single(e, s0, n)
         for s0, n in HEAD_PIECES:
+            if s0 + n == SPLIT:
+                gather_pair(0, 2 * C, SPLIT - 2 * C, 384)
             gather_pair(1, s0, n)
             nc.gpsimd.tensor_copy(**interleave(s0, n, 0, n))
         for s0, n in TAIL_PIECES:

@@ -24,7 +24,7 @@ LOAD_WIDTH = 256
 TOKEN_LOADS = ((0, LOAD_WIDTH), (256, LOAD_WIDTH), (512, 128))
 TOKEN_GROUPS = tuple((t0, 128) for t0 in range(0, T, 128))
 LAST_GROUP_ON_VECTOR = 96
-SINGLES_ON_VECTOR = 192
+SINGLES_ON_VECTOR = 256
 SPLIT = 640
 HEAD_PIECES = ((0, P), (P, C), (P + C, C))
 TAIL_PIECES = ((SPLIT, C + P), (4 * C, C))
@@ -147,7 +147,7 @@ def tile_moe_prv_lin_none_kernel(tc, uT, wu, w_words, w_scales, gate, offs, pos1
         nc.scalar.copy(**project(0, range(0, 2), bank(0, "x0_a")[:]))
         shared = [bank(3, "x_shared0"), bank(4, "x_shared1")]
         nc.vector.tensor_copy(**project(1, range(0, 1), bank(5, "x1_a")[:, 0:256]))
-        nc.vector.tensor_copy(**project(0, range(2, 3), bank(1, "x0_b")[:, 0:256]))
+        nc.scalar.copy(**project(0, range(2, 3), bank(1, "x0_b")[:, 0:256]))
         nc.vector.tensor_copy(**project(0, range(3, 4), bank(2, "x0_c")[:, 0:256]))
         nc.scalar.copy(**project(0, range(4, 5), shared[0][:, 0:256]))
         nc.scalar.copy(**project(1, range(1, 5, 3), shared[1][:]))

@@ -23,7 +23,7 @@ BANK = 512
 LOAD_WIDTH = 256
 TOKEN_LOADS = ((0, LOAD_WIDTH), (256, LOAD_WIDTH), (512, 128))
 TOKEN_GROUPS = tuple((t0, 128) for t0 in range(0, T, 128))
-LAST_GROUP_ON_VECTOR = 96
+LAST_GROUP_ON_VECTOR = 64
 SINGLES_ON_VECTOR = 256
 SPLIT = 640
 HEAD_PIECES = ((0, P), (P, C), (P + C, C))

@@ -200,13 +200,12 @@ def tile_moe_prv_lin_none_kernel(tc, uT, wu, w_words, w_scales, gate, offs, pos1
                 )
             return dict(out=y_sb[i][:, s0 : s0 + n], in_=sums)
 
-        gather_pair(0, 0, 2 * C, 64)
+        gather_pair(0, 0, SPLIT // 2)
+        gather_pair(0, SPLIT // 2, SPLIT // 2)
         for s0, n in TAIL_PIECES:
             for e in range(2):
                 gather_single(e, s0, n)
         for s0, n in HEAD_PIECES:
-            if s0 + n == SPLIT:
-                gather_pair(0, 2 * C, SPLIT - 2 * C, 384)
             gather_pair(1, s0, n)
             nc.gpsimd.tensor_copy(**interleave(s0, n, 0, n))
         for s0, n in TAIL_PIECES:

@@ -25,9 +25,9 @@ TOKEN_LOADS = ((0, LOAD_WIDTH), (256, LOAD_WIDTH), (512, 128))
 TOKEN_GROUPS = tuple((t0, 128) for t0 in range(0, T, 128))
 LAST_GROUP_ON_VECTOR = 64
 SINGLES_ON_VECTOR = 256
-SPLIT = 640
-HEAD_PIECES = ((0, P), (P, C), (P + C, C))
-TAIL_PIECES = ((SPLIT, C + P), (4 * C, C))
+SPLIT = 608
+HEAD_PIECES = ((0, P), (P, C), (P + C, SPLIT - P - C))
+TAIL_PIECES = ((SPLIT, 4 * C - SPLIT), (4 * C, C))
 SLOT_GROUPS = ((0, C), (C, C), (2 * C, C), (3 * C, C), (4 * C, P), (4 * C + P, P))
 CUT = 384
 
@@ -200,8 +200,8 @@ def tile_moe_prv_lin_none_kernel(tc, uT, wu, w_words, w_scales, gate, offs, pos1
                 )
             return dict(out=y_sb[i][:, s0 : s0 + n], in_=sums)
 
-        gather_pair(0, 0, SPLIT // 2)
-        gather_pair(0, SPLIT // 2, SPLIT // 2)
+        gather_pair(0, 0, 320)
+        gather_pair(0, 320, SPLIT - 320)
         for s0, n in TAIL_PIECES:
             for e in range(2):
                 gather_single(e, s0, n)
@@ -210,7 +210,7 @@ def tile_moe_prv_lin_none_kernel(tc, uT, wu, w_words, w_scales, gate, offs, pos1
             nc.gpsimd.tensor_copy(**interleave(s0, n, 0, n))
         for s0, n in TAIL_PIECES:
             gather_pair(1, s0, n)
-            for a, b in ((0, P), (P, n)):
+            for a, b in ((0, n - C), (n - C, n)) if n > C else ((0, P), (P, n)):
                 nc.scalar.copy(**interleave(s0, n, a, b))
         xs_codes = keep.tile([P, S], U32, name="xs_codes", tag="xs_head", align_bytes=64)
         for s0, n in SLOT_GROUPS:

from contextlib import ExitStack

import concourse.mybir as mybir
from concourse.masks import make_identity

K, T, E, C, N, M = 512, 640, 5, 256, 384, 512
S = E * C
FLOPS = 2 * M * K * T + 2 * K * N * S

F32 = mybir.dt.float32
BF16 = mybir.dt.bfloat16
I32 = mybir.dt.int32
U32 = mybir.dt.uint32
U16 = mybir.dt.uint16
U8 = mybir.dt.uint8
FP8X4 = mybir.dt.float8_e4m3fn_x4
MULT = mybir.AluOpType.mult
ADD = mybir.AluOpType.add
COPY = mybir.ActivationFunctionType.Copy

P = 128
BANK = 512
LOAD_WIDTH = 256
TOKEN_LOADS = ((0, LOAD_WIDTH), (256, LOAD_WIDTH), (512, 128))
TOKEN_GROUPS = tuple((t0, 128) for t0 in range(0, T, 128))
LAST_GROUP_ON_VECTOR = 64
SINGLES_ON_VECTOR = 256
SPLIT = 608
HEAD_PIECES = ((0, P), (P, C), (P + C, SPLIT - P - C))
TAIL_PIECES = ((SPLIT, 4 * C - SPLIT), (4 * C, C))
SLOT_GROUPS = ((0, C), (C, C), (2 * C, C), (3 * C, C), (4 * C, P), (4 * C + P, P))
CUT = 384


def tile_moe_prv_lin_none_kernel(tc, uT, wu, w_words, w_scales, gate, offs, pos1, pos2, out):
    nc = tc.nc
    with ExitStack() as ctx:
        keep = ctx.enter_context(tc.tile_pool(name="keep", bufs=1))
        psum = ctx.enter_context(tc.psum_pool(name="psum", bufs=1))

        def bank(b, name):
            return psum.tile([P, BANK], F32, name=name, tag="bank%d" % b)

        wu_rows = wu.rearrange("(p j) c -> p j c", j=4)
        wu_raw = [keep.tile([P, 2, K], F32, name="wu_raw%d" % h) for h in range(2)]
        for h in range(2):
            nc.sync.dma_start(out=wu_raw[h][:], in_=wu_rows[:, 2 * h : 2 * h + 2, :])
        u_rows = uT.rearrange("(p j) t -> p j t", j=4)
        u_raw = [keep.tile([P, 4, w], F32, name="u_raw%d" % c, tag="u_raw%d" % c, align_bytes=32) for c, (t0, w) in enumerate(TOKEN_LOADS)]
        for c, (t0, w) in enumerate(TOKEN_LOADS):
            nc.sync.dma_start(out=u_raw[c][:], in_=u_rows[:, :, t0 : t0 + w])
        offs_sb = keep.tile([P, S // 16], U16, name="offs_sb")
        nc.sync.dma_start(offs_sb[:], offs)

        w_codes = keep.tile([P, E, N], U32, name="w_codes", align_bytes=64)
        nc.sync.dma_start(
            out=w_codes[:].bitcast(I32),
            in_=w_words[:, 0, :, :, :].rearrange("e p n r -> p e (n r)").bitcast(I32),
        )
        w_scale = keep.tile([P, E, N], U8, name="w_scale", align_bytes=64)
        nc.gpsimd.memset(w_scale[:].bitcast(I32), 0)
        ident = keep.tile([P, P], F32, name="ident")
        make_identity(nc, ident[:])
        for q in range(4):
            nc.sync.dma_start(
                out=w_scale[32 * q : 32 * q + 4, :, :].bitcast(I32),
                in_=w_scales[:, 0, 4 * q : 4 * q + 4, :].rearrange("e q n -> q e n").bitcast(I32),
            )
        pos1_sb = keep.tile([P, T // 16], U16, name="pos1_sb")
        nc.sync.dma_start(pos1_sb[:], pos1)
        pos2_sb = keep.tile([P, T // 16], U16, name="pos2_sb")
        nc.sync.dma_start(pos2_sb[:], pos2)
        gate_sb = keep.tile([P, 2, T], F32, name="gate_sb")
        nc.sync.dma_start(out=gate_sb[:], in_=gate[:, 0:P, :].rearrange("r p t -> p r t"))
        gate_col = keep.tile([P, T // P], F32, name="gate_col")
        with nc.allow_non_contiguous_dma(reason="one weight a partition"):
            nc.sync.dma_start(out=gate_col[:], in_=gate[0, 0, :].rearrange("(b p) -> p b", p=P))

        x_all = keep.tile([P, 4 * T], BF16, name="x_all", tag="u_raw2", align_bytes=32)
        x_pairs = [x_all[:, 2 * T * u : 2 * T * (u + 1)].rearrange("p (t e) -> p t e", e=2) for u in range(2)]
        wu_bf = [keep.tile([P, 2, P, 4], BF16, name="wu_bf%d" % u, align_bytes=64) for u in range(2)]
        wu_codes = [keep.tile([P, 2, P], U32, name="wu_codes%d" % u, align_bytes=64) for u in range(2)]
        wu_scale = [keep.tile([P, 2, P], U8, name="wu_scale%d" % u, align_bytes=64) for u in range(2)]

        def wu_views(u, h):
            return dict(
                out=wu_bf[u][:].rearrange("p e m j -> p m j e")[:, :, 2 * h : 2 * h + 2, :],
                in_=wu_raw[h][:].rearrange("p j (m t) -> p m j t", t=4)[:, :, :, 2 * u : 2 * u + 2],
            )

        def wu_quantize(u):
            nc.vector.quantize_mx(
                out=wu_codes[u][:].rearrange("p e m -> p (e m)").bitcast(FP8X4),
                scales=wu_scale[u][:].rearrange("p e m -> p (e m)"),
                in_=wu_bf[u][:].rearrange("p e m j -> p (e m j)"),
            )

        u_bf = [keep.tile([P, w, 4], BF16, name="u_bf%d" % c, align_bytes=64) for c, (t0, w) in enumerate(TOKEN_GROUPS)]
        u_codes = keep.tile([P, T], U32, name="u_codes", align_bytes=64)
        u_scale = keep.tile([P, T], U8, name="u_scale", align_bytes=64)

        def u_views(c, a, b):
            load, lo = divmod(TOKEN_GROUPS[c][0], LOAD_WIDTH)
            return dict(
                out=u_bf[c][:, a:b, :].rearrange("p (g i) j -> p g j i", i=4),
                in_=u_raw[load][:, :, lo + a : lo + b].rearrange("p j (g i) -> p g j i", i=4),
            )

        def u_quantize(c):
            t0, w = TOKEN_GROUPS[c]
            nc.vector.quantize_mx(
                out=u_codes[:, t0 : t0 + w].bitcast(FP8X4),
                scales=u_scale[:, t0 : t0 + w],
                in_=u_bf[c][:].rearrange("p w j -> p (w j)"),
            )

        def project(u, groups, sums):
            for n, c in enumerate(groups):
                for e in range(2):
                    nc.tensor.matmul_mx(
                        out=sums[:, (2 * n + e) * P : (2 * n + e + 1) * P],
                        lhsT=wu_codes[u][:, e, :].bitcast(FP8X4),
                        lhsT_scale=wu_scale[u][:, e, :],
                        rhs=u_codes[:, P * c : P * (c + 1)].bitcast(FP8X4),
                        rhs_scale=u_scale[:, P * c : P * (c + 1)],
                        start=True,
                        stop=True,
                    )
            by_group = x_pairs[u].rearrange("p (c t) e -> p c t e", t=P)
            return dict(out=by_group[:, slice(groups.start, groups.stop, groups.step), :, :], in_=sums.rearrange("p (c e t) -> p c t e", e=2, t=P))

        for h in range(2):
            nc.vector.tensor_copy(**wu_views(0, h))
            nc.scalar.copy(**wu_views(1, h))
        wu_quantize(0)
        wu_quantize(1)
        for c in (0, 2):
            nc.vector.tensor_copy(**u_views(c, 0, P))
            nc.scalar.copy(**u_views(c + 1, 0, P))
            u_quantize(c)
            if c == 0:
                u_quantize(1)
        nc.vector.tensor_copy(**u_views(4, 0, LAST_GROUP_ON_VECTOR))
        nc.scalar.copy(**u_views(4, LAST_GROUP_ON_VECTOR, P))
        u_quantize(3)
        u_quantize(4)
        nc.scalar.copy(**project(0, range(0, 2), bank(0, "x0_a")[:]))
        shared = [bank(3, "x_shared0"), bank(4, "x_shared1")]
        nc.vector.tensor_copy(**project(1, range(0, 1), bank(5, "x1_a")[:, 0:256]))
        nc.scalar.copy(**project(0, range(2, 3), bank(1, "x0_b")[:, 0:256]))
        nc.vector.tensor_copy(**project(0, range(3, 4), bank(2, "x0_c")[:, 0:256]))
        nc.scalar.copy(**project(0, range(4, 5), shared[0][:, 0:256]))
        nc.scalar.copy(**project(1, range(1, 5, 3), shared[1][:]))
        nc.scalar.copy(**project(1, range(2, 4), bank(1, "x1_b")[:]))
        x_single = keep.tile([P, 2, T], BF16, name="x_single")
        nc.vector.tensor_copy(out=x_single[:, :, 0:SINGLES_ON_VECTOR], in_=x_pairs[0][:, 0:SINGLES_ON_VECTOR, :].rearrange("p t e -> p e t"))
        for e in range(2):
            nc.gpsimd.tensor_copy(out=x_single[:, e, SINGLES_ON_VECTOR:T], in_=x_pairs[0][:, SINGLES_ON_VECTOR:T, e])

        xs_head = keep.tile([P, 2, SPLIT], U32, name="xs_head", tag="xs_head", align_bytes=64)
        xs_tail = {s0: keep.tile([P, 2 * n], U32, name="xs_tail%d" % s0) for s0, n in TAIL_PIECES}
        xs_bf = keep.tile([P, S, 4], BF16, name="xs_bf", align_bytes=64)
        xs_scale = keep.tile([P, S], U8, name="xs_scale", align_bytes=64)

        def gathered(s0, n):
            return xs_head[:, :, s0 : s0 + n] if s0 < SPLIT else xs_tail[s0][:].rearrange("p (u s) -> p u s", u=2)

        def gather_pair(u, s0, n, spare=0):
            window = x_all[:, 2 * T * u : 2 * (T * (u + 1) + spare)].bitcast(U32)
            nc.vector.tensor_copy(gathered(s0, n)[:, u, :], window.indirect(offs_sb[:, s0 // 16 : (s0 + n) // 16]))

        def gather_single(e, s0, n):
            halves = gathered(s0, n)[:, 0, :].bitcast(BF16).rearrange("p (s e) -> p s e", e=2)
            nc.scalar.activation(halves[:, :, e], x_single[:, e, :].indirect(offs_sb[:, s0 // 16 : (s0 + n) // 16]), COPY)

        def interleave(s0, n, a, b):
            words = xs_bf[:].rearrange("p s j -> p (s j)").bitcast(U32).rearrange("p (s u) -> p s u", u=2)
            return dict(out=words[:, s0 + a : s0 + b, :], in_=gathered(s0, n).rearrange("p u s -> p s u")[:, a:b, :])

        def xs_quantize(s0, n):
            nc.vector.quantize_mx(
                out=xs_codes[:, s0 : s0 + n].bitcast(FP8X4),
                scales=xs_scale[:, s0 : s0 + n],
                in_=xs_bf[:, s0 : s0 + n, :].rearrange("p s j -> p (s j)"),
            )

        y_sb = [keep.tile([P, S], F32, name="y_sb%d" % i) for i in range(N // P)]

        def experts(i, s0, n, step, sums):
            for a in range(0, n, step):
                ex = (s0 + a) // C
                nc.tensor.matmul_mx(
                    out=sums[:, a : a + step],
                    lhsT=w_codes[:, ex, P * i : P * (i + 1)].bitcast(FP8X4),
                    lhsT_scale=w_scale[:, ex, P * i : P * (i + 1)],
                    rhs=xs_codes[:, s0 + a : s0 + a + step].bitcast(FP8X4),
                    rhs_scale=xs_scale[:, s0 + a : s0 + a + step],
                    start=True,
                    stop=True,
                )
            return dict(out=y_sb[i][:, s0 : s0 + n], in_=sums)

        gather_pair(0, 0, 320)
        gather_pair(0, 320, SPLIT - 320)
        for s0, n in TAIL_PIECES:
            for e in range(2):
                gather_single(e, s0, n)
        for s0, n in HEAD_PIECES:
            gather_pair(1, s0, n)
            nc.gpsimd.tensor_copy(**interleave(s0, n, 0, n))
        for s0, n in TAIL_PIECES:
            gather_pair(1, s0, n)
            for a, b in ((0, n - C), (n - C, n)) if n > C else ((0, P), (P, n)):
                nc.scalar.copy(**interleave(s0, n, a, b))
        xs_codes = keep.tile([P, S], U32, name="xs_codes", tag="xs_head", align_bytes=64)
        for s0, n in SLOT_GROUPS:
            xs_quantize(s0, n)
        for ex in (0, 1):
            nc.scalar.copy(**experts(0, ex * C, C, C, bank(ex, "y0_%d" % ex)[:, 0:C]))
        for ex in (2, 3):
            nc.vector.tensor_copy(**experts(0, ex * C, C, C, bank(ex, "y0_%d" % ex)[:, 0:C]))
        nc.scalar.copy(**experts(0, 4 * C, P, P, bank(4, "y0_4")[:, 0:P]))
        nc.scalar.copy(**experts(0, 4 * C + P, P, P, bank(5, "y0_5")[:, 0:P]))

        def empty(i, s0, n, b):
            nc.scalar.copy(**experts(i, s0, n, C, bank(b, "y%d_%d" % (i, s0))[:, 0:n]))

        lists = (pos1_sb, pos2_sb)
        out_rows = out.rearrange("(i p) t -> p i t", p=P)
        last = T // P - 1
        second = keep.tile([P, 2, T], F32, name="second")
        plain = keep.tile([P, 2, T], F32, name="plain")

        def fetch(i, r, t0, t1, term):
            nc.vector.tensor_tensor(term, y_sb[i][:].indirect(lists[r][:, t0 // 16 : t1 // 16]), gate_sb[:, r, t0:t1], MULT)

        def fetch_plain(i, t0, t1):
            nc.scalar.activation(plain[:, i - 1, t0:t1], y_sb[i][:].indirect(pos1_sb[:, t0 // 16 : t1 // 16]), COPY)

        def weigh(b, n, banks, turned):
            there = bank(banks[0], "there%d" % b)[:, 0 : n * P]
            back = bank(banks[1], "back%d" % b)[:, 0 : n * P]
            for i in range(n):
                nc.tensor.transpose(there[:, P * i : P * (i + 1)], plain[:, i, P * b : P * (b + 1)], ident[:])
            nc.scalar.activation(turned, there, COPY, scale=gate_col[:, b : b + 1])
            for i in range(n):
                nc.tensor.transpose(back[:, P * i : P * (i + 1)], turned[:, P * i : P * (i + 1)], ident[:])
            return back.rearrange("p (i t) -> p i t", i=n)

        def add_and_store(i0, i1, t0, t1, first, other, engine=nc.vector):
            total = keep.tile([P, i1 - i0, t1 - t0], F32, name="total%d_%d" % (i0, t0))
            engine.tensor_tensor(total[:], first, other, ADD)
            nc.sync.dma_start(out=out_rows[:, i0:i1, t0:t1], in_=total[:])

        terms0 = keep.tile([P, 2, T], F32, name="terms0")
        fetch(0, 1, 0, T, terms0[:, 1, :])
        for t0, t1 in ((0, CUT), (CUT, T)):
            fetch(0, 0, t0, t1, terms0[:, 0, t0:t1])
        for t0, t1 in ((0, CUT), (CUT, T)):
            add_and_store(0, 1, t0, t1, terms0[:, 0:1, t0:t1], terms0[:, 1:2, t0:t1])

        for s0, n, b in ((0, C, 1), (C, BANK, 6), (C + BANK, BANK, 7)):
            empty(1, s0, n, b)
        empty(2, 0, BANK, 0)
        fetch_plain(1, 0, T)
        empty(2, BANK, BANK, 2)
        empty(2, 2 * BANK, C, 3)
        turned = keep.tile([P, T // P, 2 * P], F32, name="turned")
        fetch(1, 1, 0, T, second[:, 0, :])
        weighed = {last: weigh(last, 1, (4, 5), turned[:, last, 0:P])}
        fetch_plain(2, 0, 2 * P)
        fetch_plain(2, 2 * P, last * P)
        for b, banks in enumerate(((6, 4), (7, 2), (0, 3), (1, 6))):
            weighed[b] = weigh(b, 2, banks, turned[:, b, :])
        fetch(2, 1, 0, T, second[:, 1, :])
        first_end = keep.tile([P, 1, P], F32, name="first_end")
        fetch(2, 0, last * P, T, first_end[:, 0, :])
        add_and_store(1, 2, last * P, T, weighed[last], second[:, 0:1, last * P : T])
        for b in range(last - 1):
            add_and_store(1, 3, P * b, P * (b + 1), weighed[b], second[:, :, P * b : P * (b + 1)])
            if b == 0:
                add_and_store(2, 3, last * P, T, first_end[:], second[:, 1:2, last * P : T], nc.gpsimd)
        for i in (1, 2):
            add_and_store(i, i + 1, (last - 1) * P, last * P, weighed[last - 1][:, i - 1 : i, :], second[:, i - 1 : i, (last - 1) * P : last * P])
